import numpy as np
import ml_dtypes


def mxq(x, axis, fmt="e4m3"):
    dtype, down = {"e4m3": (ml_dtypes.float8_e4m3fn, 7), "e5m2": (ml_dtypes.float8_e5m2, 14)}[fmt]
    v = np.moveaxis(np.asarray(x, np.float32).astype(ml_dtypes.bfloat16).astype(np.float64), axis, -1)
    blocks = v.reshape(v.shape[:-1] + (-1, 32))
    amax = np.abs(blocks).max(-1, keepdims=True)
    byte = np.maximum(np.where(amax > 0, np.frexp(amax)[1] - 1 + 127, 0) - down, 1)
    scale = np.exp2(byte - 127.0)
    codes = (blocks / scale).astype(np.float32).astype(dtype).astype(np.float64)
    return np.moveaxis((codes * scale).reshape(v.shape), -1, axis)


WIDE = False


def mx_kscale(k):
    if not WIDE:
        return np.ones(k)
    levels = np.array([10, -10, 5, -5, 0])
    if k % 512:
        return np.exp2(np.random.permutation(np.resize(levels, k // 32))).repeat(32)
    a = np.empty((k // 512, 16))
    for p in range(k // 512):
        a[p, :8] = np.random.permutation(np.resize(levels, 8))
        for g in range(8):
            far = levels[np.abs(levels - a[p, g]) >= 10]
            a[p, g + 8] = far[np.random.randint(len(far))]
    return np.exp2(a.ravel()).repeat(32)


def f64(x):
    return np.asarray(x).astype(np.float64)


def striped(idx):
    return np.tile(idx.reshape(-1, 16).T, (8, 1)).astype(np.uint16)


def unstriped(offs):
    return offs[:16].T.reshape(-1).astype(np.int64)


E2M1 = np.array([0.0, 0.5, 1.0, 1.5, 2.0, 3.0, 4.0, 6.0, -0.0, -0.5, -1.0, -1.5, -2.0, -3.0, -4.0, -6.0])


def pack_fp4(w):
    k, n = w.shape
    w = f64(np.asarray(w, np.float32).astype(ml_dtypes.bfloat16)).reshape(k // 32, 32, n)
    amax = np.abs(w).max(1)
    mant, ex = np.frexp(amax / 6.0)
    byte = np.clip(np.where(amax > 0, np.where(mant > 0.5, ex, ex - 1) + 127, 1), 1, 254)
    scaled = (w * np.exp2(127.0 - byte)[:, None, :]).reshape(k, n).astype(np.float32)
    c = np.ascontiguousarray(scaled.reshape(k // 512, 128, 4, n).transpose(0, 1, 3, 2)).astype(ml_dtypes.float4_e2m1fn).view(np.uint8) & 0xF
    words = (c[..., 0::2] | (c[..., 1::2] << 4)).reshape(k // 512, 128, 2 * n)
    return np.ascontiguousarray(words), np.ascontiguousarray(byte.astype(np.uint8).reshape(k // 512, 16, n))


def unpack_fp4(words, scales):
    g, _, n = scales.shape
    words = np.ascontiguousarray(words).reshape(g, 128, n, 2)
    nib = np.empty((g, 128, n, 4), np.uint8)
    nib[..., 0::2] = words & 0xF
    nib[..., 1::2] = words >> 4
    vals = E2M1[nib] * np.repeat(np.exp2(scales.astype(np.float64) - 127.0), 8, axis=1)[..., None]
    return vals.transpose(0, 1, 3, 2).reshape(g * 512, n)


K, T, S, N = 512, 4096, 1024, 128


def setup_inputs():
    n = np.random.standard_normal
    s = mx_kscale(K)[:, None]
    packed_w1 = pack_fp4(n((K, N)) / np.sqrt(K) / s)
    packed_w2 = pack_fp4(n((K, N)) / np.sqrt(K) / s)
    packed_w3 = pack_fp4(n((K, N)) / np.sqrt(K) / s)
    return {
        "xT": (n((K, T)) * s).astype(np.float32),
        "w1_words": packed_w1[0],
        "w1_scales": packed_w1[1],
        "w2_words": packed_w2[0],
        "w2_scales": packed_w2[1],
        "w3_words": packed_w3[0],
        "w3_scales": packed_w3[1],
        "offs": striped(np.random.permutation(T)[:S]),
    }


def reference(xT, w1_words, w1_scales, w2_words, w2_scales, w3_words, w3_scales, offs):
    xq = mxq(f64(xT)[:, unstriped(offs)], 0, "e4m3")
    return np.maximum(np.maximum(unpack_fp4(w1_words, w1_scales).T @ xq, unpack_fp4(w2_words, w2_scales).T @ xq), unpack_fp4(w3_words, w3_scales).T @ xq)

@@ -1,0 +1,109 @@
+from contextlib import ExitStack
+
+import concourse.mybir as mybir
+
+K, T, S, N = 512, 4096, 1024, 128
+FLOPS = 2 * 3 * K * N * S
+
+F32 = mybir.dt.float32
+BF16 = mybir.dt.bfloat16
+I32 = mybir.dt.int32
+U32 = mybir.dt.uint32
+U16 = mybir.dt.uint16
+U8 = mybir.dt.uint8
+FP8X4 = mybir.dt.float8_e4m3fn_x4
+FP4X4 = mybir.dt.float4_e2m1fn_x4
+COPY = mybir.ActivationFunctionType.Copy
+MAX = mybir.AluOpType.max
+
+P = 128
+PACK = 4
+HALF = S // 2
+CHUNK = 256
+LAST_PIECES = ((1280, "scalar"), (1280, "scalar"), (1024, "vector"), (512, "scalar"))
+
+
+def tile_picked_maxout_max_e_kernel(tc, xT, w1_words, w1_scales, w2_words, w2_scales, w3_words, w3_scales, offs, out):
+    nc = tc.nc
+    rows = xT.rearrange("(p j) t -> p j t", j=PACK)
+    with ExitStack() as ctx:
+        keep = ctx.enter_context(tc.tile_pool(name="keep", bufs=1))
+        psum = ctx.enter_context(tc.psum_pool(name="psum", bufs=1))
+
+        offsets = keep.tile([P, S // 16], U16, name="offsets")
+        planes = [keep.tile([P, T], F32, name=f"plane{j}") for j in range(PACK)]
+        last_bf = keep.tile([P, T], BF16, name="last_bf")
+        picked = [keep.tile([P, HALF, PACK], BF16, name=f"picked{h}", align_bytes=64) for h in range(2)]
+        half_offs = [offsets[:, h * (HALF // 16) : (h + 1) * (HALF // 16)] for h in range(2)]
+
+        warm = keep.tile([P, 8], BF16, name="warm")
+        warm2 = keep.tile([P, 8], BF16, name="warm2")
+        nc.vector.memset(warm[:], 0.0)
+        nc.scalar.activation(warm2[:], warm[:], COPY)
+
+        nc.sync.dma_start(planes[0][:], rows[:, 0, :])
+        nc.sync.dma_start(offsets[:], offs)
+        for j in range(1, PACK - 1):
+            nc.sync.dma_start(planes[j][:], rows[:, j, :])
+        c0 = 0
+        for width, engine in LAST_PIECES:
+            nc.sync.dma_start(planes[PACK - 1][:, c0 : c0 + width], rows[:, PACK - 1, c0 : c0 + width])
+            c0 = c0 + width
+
+        w_codes = keep.tile([P, 3 * 2 * N], U8, name="w_codes", align_bytes=64)
+        w_bytes = keep.tile([P, 3 * N], U8, name="w_bytes", align_bytes=64)
+        nc.gpsimd.memset(w_bytes[:].bitcast(I32), 0)
+        for i, (words, scales) in enumerate(((w1_words, w1_scales), (w2_words, w2_scales), (w3_words, w3_scales))):
+            nc.gpsimd.dma_start(w_codes[:, i * 2 * N : (i + 1) * 2 * N].bitcast(I32), words[0].bitcast(I32))
+            for q in range(4):
+                nc.gpsimd.dma_start(
+                    w_bytes[32 * q : 32 * q + 4, i * N : (i + 1) * N].bitcast(I32),
+                    scales[0, 4 * q : 4 * q + 4, :].bitcast(I32),
+                )
+
+        for j in range(PACK - 1):
+            for h in range(2):
+                nc.vector.tensor_copy(picked[h][:, :, j], planes[j][:].indirect(half_offs[h]))
+
+        c0 = 0
+        for width, engine in LAST_PIECES:
+            cols = slice(c0, c0 + width)
+            if engine == "scalar":
+                nc.scalar.activation(last_bf[:, cols], planes[PACK - 1][:, cols], COPY)
+            else:
+                nc.vector.tensor_copy(last_bf[:, cols], planes[PACK - 1][:, cols])
+            c0 = c0 + width
+
+        nc.vector.tensor_copy(picked[0][:, :, PACK - 1], planes[PACK - 1][:].indirect(half_offs[0]))
+        nc.scalar.activation(picked[1][:, :, PACK - 1], last_bf[:].indirect(half_offs[1]), COPY)
+
+        accs = []
+        for c in range(S // CHUNK):
+            h, r = divmod(c * CHUNK, HALF)
+            codes = keep.tile([P, CHUNK], U32, name=f"codes{c}", align_bytes=64)
+            scale = keep.tile([P, CHUNK], U8, name=f"scale{c}", align_bytes=64)
+            nc.vector.quantize_mx(
+                out=codes[:].bitcast(FP8X4),
+                scales=scale[:],
+                in_=picked[h][:, r : r + CHUNK, :].rearrange("p n j -> p (n j)"),
+            )
+            acc = []
+            for i in range(3):
+                bank = psum.tile([P, CHUNK], F32, name=f"acc{i}", tag=f"acc{i}", bufs=(2, 3, 3)[i])
+                nc.tensor.matmul_mx(
+                    out=bank[:],
+                    lhsT=w_codes[:, i * 2 * N : (i + 1) * 2 * N].bitcast(FP4X4),
+                    lhsT_scale=w_bytes[:, i * N : (i + 1) * N],
+                    rhs=codes[:].bitcast(FP8X4),
+                    rhs_scale=scale[:],
+                    start=True,
+                    stop=True,
+                )
+                acc.append(bank)
+            first = keep.tile([P, CHUNK], F32, name=f"first{c}")
+            second = keep.tile([P, CHUNK], F32, name=f"second{c}")
+            best = keep.tile([P, CHUNK], F32, name=f"best{c}")
+            nc.scalar.activation(first[:], acc[0][:], COPY)
+            nc.vector.tensor_tensor(second[:], acc[1][:], first[:], MAX)
+            nc.vector.tensor_tensor(best[:], acc[2][:], second[:], MAX)
+            nc.sync.dma_start(out[:, c * CHUNK : (c + 1) * CHUNK], best[:])

@@ -41,25 +41,24 @@ def tile_picked_maxout_max_e_kernel(tc, xT, w1_words, w1_scales, w2_words, w2_sc
         nc.vector.memset(warm[:], 0.0)
         nc.scalar.activation(warm2[:], warm[:], COPY)
 
-        nc.sync.dma_start(planes[0][:], rows[:, 0, :])
+        w_codes = keep.tile([P, 3 * 2 * N], U8, name="w_codes", align_bytes=64)
+        w_bytes = keep.tile([P, 3 * N], U8, name="w_bytes", align_bytes=64)
+        staged = keep.tile([16, 3 * N], U8, name="staged", align_bytes=64)
+        nc.vector.memset(w_bytes[:].bitcast(I32), 0)
+
         nc.sync.dma_start(offsets[:], offs)
-        for j in range(1, PACK - 1):
+        for i, scales in enumerate((w1_scales, w2_scales, w3_scales)):
+            nc.scalar.dma_start(staged[:, i * N : (i + 1) * N].bitcast(I32), scales[0].bitcast(I32))
+        for i, words in enumerate((w1_words, w2_words, w3_words)):
+            nc.scalar.dma_start(w_codes[:, i * 2 * N : (i + 1) * 2 * N].bitcast(I32), words[0].bitcast(I32))
+        for j in range(PACK - 1):
             nc.sync.dma_start(planes[j][:], rows[:, j, :])
         c0 = 0
         for width, engine in LAST_PIECES:
             nc.sync.dma_start(planes[PACK - 1][:, c0 : c0 + width], rows[:, PACK - 1, c0 : c0 + width])
             c0 = c0 + width
-
-        w_codes = keep.tile([P, 3 * 2 * N], U8, name="w_codes", align_bytes=64)
-        w_bytes = keep.tile([P, 3 * N], U8, name="w_bytes", align_bytes=64)
-        nc.gpsimd.memset(w_bytes[:].bitcast(I32), 0)
-        for i, (words, scales) in enumerate(((w1_words, w1_scales), (w2_words, w2_scales), (w3_words, w3_scales))):
-            nc.gpsimd.dma_start(w_codes[:, i * 2 * N : (i + 1) * 2 * N].bitcast(I32), words[0].bitcast(I32))
-            for q in range(4):
-                nc.gpsimd.dma_start(
-                    w_bytes[32 * q : 32 * q + 4, i * N : (i + 1) * N].bitcast(I32),
-                    scales[0, 4 * q : 4 * q + 4, :].bitcast(I32),
-                )
+        for q in range(4):
+            nc.sync.dma_start(w_bytes[32 * q : 32 * q + 4, :].bitcast(I32), staged[4 * q : 4 * q + 4, :].bitcast(I32))
 
         for j in range(PACK - 1):
             for h in range(2):

@@ -20,7 +20,7 @@ P = 128
 PACK = 4
 HALF = S // 2
 CHUNK = 256
-LAST_PIECES = ((1280, "scalar"), (1280, "scalar"), (1024, "vector"), (512, "scalar"))
+LAST_PIECES = ((1408, "scalar"), (1408, "scalar"), (768, "vector"), (512, "scalar"))
 
 
 def tile_picked_maxout_max_e_kernel(tc, xT, w1_words, w1_scales, w2_words, w2_scales, w3_words, w3_scales, offs, out):
@@ -36,23 +36,25 @@ def tile_picked_maxout_max_e_kernel(tc, xT, w1_words, w1_scales, w2_words, w2_sc
         picked = [keep.tile([P, HALF, PACK], BF16, name=f"picked{h}", align_bytes=64) for h in range(2)]
         half_offs = [offsets[:, h * (HALF // 16) : (h + 1) * (HALF // 16)] for h in range(2)]
 
-        warm = keep.tile([P, 8], BF16, name="warm")
-        warm2 = keep.tile([P, 8], BF16, name="warm2")
-        nc.vector.memset(warm[:], 0.0)
-        nc.scalar.activation(warm2[:], warm[:], COPY)
-
         w_codes = keep.tile([P, 3 * 2 * N], U8, name="w_codes", align_bytes=64)
         w_bytes = keep.tile([P, 3 * N], U8, name="w_bytes", align_bytes=64)
         staged = keep.tile([16, 3 * N], U8, name="staged", align_bytes=64)
         nc.vector.memset(w_bytes[:].bitcast(I32), 0)
 
+        all_words = (w1_words, w2_words, w3_words)
+
+        def load_words(i):
+            nc.sync.dma_start(w_codes[:, i * 2 * N : (i + 1) * 2 * N].bitcast(I32), all_words[i][0].bitcast(I32))
+
+        nc.sync.dma_start(planes[0][:], rows[:, 0, :])
         nc.sync.dma_start(offsets[:], offs)
+        nc.sync.dma_start(planes[1][:], rows[:, 1, :])
         for i, scales in enumerate((w1_scales, w2_scales, w3_scales)):
-            nc.scalar.dma_start(staged[:, i * N : (i + 1) * N].bitcast(I32), scales[0].bitcast(I32))
-        for i, words in enumerate((w1_words, w2_words, w3_words)):
-            nc.scalar.dma_start(w_codes[:, i * 2 * N : (i + 1) * 2 * N].bitcast(I32), words[0].bitcast(I32))
-        for j in range(PACK - 1):
-            nc.sync.dma_start(planes[j][:], rows[:, j, :])
+            nc.sync.dma_start(staged[:, i * N : (i + 1) * N].bitcast(I32), scales[0].bitcast(I32))
+        load_words(0)
+        load_words(1)
+        nc.sync.dma_start(planes[2][:], rows[:, 2, :])
+        load_words(2)
         c0 = 0
         for width, engine in LAST_PIECES:
             nc.sync.dma_start(planes[PACK - 1][:, c0 : c0 + width], rows[:, PACK - 1, c0 : c0 + width])
@@ -76,33 +78,37 @@ def tile_picked_maxout_max_e_kernel(tc, xT, w1_words, w1_scales, w2_words, w2_sc
         nc.vector.tensor_copy(picked[0][:, :, PACK - 1], planes[PACK - 1][:].indirect(half_offs[0]))
         nc.scalar.activation(picked[1][:, :, PACK - 1], last_bf[:].indirect(half_offs[1]), COPY)
 
-        accs = []
+        per_half = HALF // CHUNK
+        codes, scale = [], []
         for c in range(S // CHUNK):
             h, r = divmod(c * CHUNK, HALF)
-            codes = keep.tile([P, CHUNK], U32, name=f"codes{c}", align_bytes=64)
-            scale = keep.tile([P, CHUNK], U8, name=f"scale{c}", align_bytes=64)
+            codes.append(keep.tile([P, CHUNK], U32, name=f"codes{c}", align_bytes=64))
+            scale.append(keep.tile([P, CHUNK], U8, name=f"scale{c}", align_bytes=64))
             nc.vector.quantize_mx(
-                out=codes[:].bitcast(FP8X4),
-                scales=scale[:],
+                out=codes[c][:].bitcast(FP8X4),
+                scales=scale[c][:],
                 in_=picked[h][:, r : r + CHUNK, :].rearrange("p n j -> p (n j)"),
             )
-            acc = []
+        for h in range(2):
+            chunks = range(h * per_half, (h + 1) * per_half)
+            best = {}
             for i in range(3):
-                bank = psum.tile([P, CHUNK], F32, name=f"acc{i}", tag=f"acc{i}", bufs=(2, 3, 3)[i])
-                nc.tensor.matmul_mx(
-                    out=bank[:],
-                    lhsT=w_codes[:, i * 2 * N : (i + 1) * 2 * N].bitcast(FP4X4),
-                    lhsT_scale=w_bytes[:, i * N : (i + 1) * N],
-                    rhs=codes[:].bitcast(FP8X4),
-                    rhs_scale=scale[:],
-                    start=True,
-                    stop=True,
-                )
-                acc.append(bank)
-            first = keep.tile([P, CHUNK], F32, name=f"first{c}")
-            second = keep.tile([P, CHUNK], F32, name=f"second{c}")
-            best = keep.tile([P, CHUNK], F32, name=f"best{c}")
-            nc.scalar.activation(first[:], acc[0][:], COPY)
-            nc.vector.tensor_tensor(second[:], acc[1][:], first[:], MAX)
-            nc.vector.tensor_tensor(best[:], acc[2][:], second[:], MAX)
-            nc.sync.dma_start(out[:, c * CHUNK : (c + 1) * CHUNK], best[:])
+                for c in chunks:
+                    bank = psum.tile([P, CHUNK], F32, name="bank", tag="bank", bufs=8)
+                    nc.tensor.matmul_mx(
+                        out=bank[:],
+                        lhsT=w_codes[:, i * 2 * N : (i + 1) * 2 * N].bitcast(FP4X4),
+                        lhsT_scale=w_bytes[:, i * N : (i + 1) * N],
+                        rhs=codes[c][:].bitcast(FP8X4),
+                        rhs_scale=scale[c][:],
+                        start=True,
+                        stop=True,
+                    )
+                    result = keep.tile([P, CHUNK], F32, name=f"best{i}_{c}")
+                    if i == 0:
+                        nc.scalar.activation(result[:], bank[:], COPY)
+                    else:
+                        nc.vector.tensor_tensor(result[:], bank[:], best[c][:], MAX)
+                    best[c] = result
+            for c in chunks:
+                nc.sync.dma_start(out[:, c * CHUNK : (c + 1) * CHUNK], best[c][:])

@@ -51,14 +51,13 @@ def tile_picked_maxout_max_e_kernel(tc, xT, w1_words, w1_scales, w2_words, w2_sc
         nc.sync.dma_start(planes[1][:], rows[:, 1, :])
         for i, scales in enumerate((w1_scales, w2_scales, w3_scales)):
             nc.sync.dma_start(staged[:, i * N : (i + 1) * N].bitcast(I32), scales[0].bitcast(I32))
-        load_words(0)
-        load_words(1)
         nc.sync.dma_start(planes[2][:], rows[:, 2, :])
-        load_words(2)
         c0 = 0
         for width, engine in LAST_PIECES:
             nc.sync.dma_start(planes[PACK - 1][:, c0 : c0 + width], rows[:, PACK - 1, c0 : c0 + width])
             c0 = c0 + width
+        for i in range(3):
+            load_words(i)
         for q in range(4):
             nc.sync.dma_start(w_bytes[32 * q : 32 * q + 4, :].bitcast(I32), staged[4 * q : 4 * q + 4, :].bitcast(I32))
 

@@ -19,8 +19,17 @@ MAX = mybir.AluOpType.max
 P = 128
 PACK = 4
 HALF = S // 2
-CHUNK = 256
-LAST_PIECES = ((1408, "scalar"), (1408, "scalar"), (768, "vector"), (512, "scalar"))
+LAST_PIECES = ((1152, 1152), (1024, 0), (0, 512), (256, 0))
+QUANT_WIDTHS = (128, 128, 256, 256, 256)
+CHUNKS = (128, 256, 256, 256, 128)
+
+
+def spans(widths):
+    out, start = [], 0
+    for width in widths:
+        out.append(slice(start, start + width))
+        start = start + width
+    return out
 
 
 def tile_picked_maxout_max_e_kernel(tc, xT, w1_words, w1_scales, w2_words, w2_scales, w3_words, w3_scales, offs, out):
@@ -32,8 +41,8 @@ def tile_picked_maxout_max_e_kernel(tc, xT, w1_words, w1_scales, w2_words, w2_sc
 
         offsets = keep.tile([P, S // 16], U16, name="offsets")
         planes = [keep.tile([P, T], F32, name=f"plane{j}") for j in range(PACK)]
-        last_bf = keep.tile([P, T], BF16, name="last_bf")
-        picked = [keep.tile([P, HALF, PACK], BF16, name=f"picked{h}", align_bytes=64) for h in range(2)]
+        last_bf = keep.tile([P, T], BF16, name="last_bf", tag="last_bf")
+        picked = [keep.tile([P, HALF, PACK], BF16, name=f"picked{h}", tag=f"picked{h}", align_bytes=64) for h in range(2)]
         half_offs = [offsets[:, h * (HALF // 16) : (h + 1) * (HALF // 16)] for h in range(2)]
 
         w_codes = keep.tile([P, 3 * 2 * N], U8, name="w_codes", align_bytes=64)
@@ -41,73 +50,73 @@ def tile_picked_maxout_max_e_kernel(tc, xT, w1_words, w1_scales, w2_words, w2_sc
         staged = keep.tile([16, 3 * N], U8, name="staged", align_bytes=64)
         nc.vector.memset(w_bytes[:].bitcast(I32), 0)
 
-        all_words = (w1_words, w2_words, w3_words)
-
-        def load_words(i):
-            nc.sync.dma_start(w_codes[:, i * 2 * N : (i + 1) * 2 * N].bitcast(I32), all_words[i][0].bitcast(I32))
-
+        last = PACK - 1
+        pieces = spans([a + b for a, b in LAST_PIECES])
         nc.sync.dma_start(planes[0][:], rows[:, 0, :])
         nc.sync.dma_start(offsets[:], offs)
-        nc.sync.dma_start(planes[1][:], rows[:, 1, :])
         for i, scales in enumerate((w1_scales, w2_scales, w3_scales)):
             nc.sync.dma_start(staged[:, i * N : (i + 1) * N].bitcast(I32), scales[0].bitcast(I32))
-        nc.sync.dma_start(planes[2][:], rows[:, 2, :])
-        c0 = 0
-        for width, engine in LAST_PIECES:
-            nc.sync.dma_start(planes[PACK - 1][:, c0 : c0 + width], rows[:, PACK - 1, c0 : c0 + width])
-            c0 = c0 + width
-        for i in range(3):
-            load_words(i)
+        for j in range(1, last):
+            nc.sync.dma_start(planes[j][:], rows[:, j, :])
         for q in range(4):
             nc.sync.dma_start(w_bytes[32 * q : 32 * q + 4, :].bitcast(I32), staged[4 * q : 4 * q + 4, :].bitcast(I32))
+        for cols in pieces:
+            nc.sync.dma_start(planes[last][:, cols], rows[:, last, cols])
+        for i, words in enumerate((w1_words, w2_words, w3_words)):
+            nc.sync.dma_start(w_codes[:, i * 2 * N : (i + 1) * 2 * N].bitcast(I32), words[0].bitcast(I32))
 
-        for j in range(PACK - 1):
+        for j in range(last):
             for h in range(2):
                 nc.vector.tensor_copy(picked[h][:, :, j], planes[j][:].indirect(half_offs[h]))
 
-        c0 = 0
-        for width, engine in LAST_PIECES:
-            cols = slice(c0, c0 + width)
-            if engine == "scalar":
-                nc.scalar.activation(last_bf[:, cols], planes[PACK - 1][:, cols], COPY)
-            else:
-                nc.vector.tensor_copy(last_bf[:, cols], planes[PACK - 1][:, cols])
-            c0 = c0 + width
+        for cols, (on_scalar, on_vector) in zip(pieces, LAST_PIECES):
+            cut = cols.start + on_scalar
+            if on_scalar:
+                nc.scalar.activation(last_bf[:, cols.start : cut], planes[last][:, cols.start : cut], COPY)
+            if on_vector:
+                nc.vector.tensor_copy(last_bf[:, cut : cols.stop], planes[last][:, cut : cols.stop])
 
-        nc.vector.tensor_copy(picked[0][:, :, PACK - 1], planes[PACK - 1][:].indirect(half_offs[0]))
-        nc.scalar.activation(picked[1][:, :, PACK - 1], last_bf[:].indirect(half_offs[1]), COPY)
+        nc.vector.tensor_copy(picked[0][:, :, last], planes[last][:].indirect(half_offs[0]))
+        nc.scalar.activation(picked[1][:, :, last], last_bf[:].indirect(half_offs[1]), COPY)
 
-        per_half = HALF // CHUNK
-        codes, scale = [], []
-        for c in range(S // CHUNK):
-            h, r = divmod(c * CHUNK, HALF)
-            codes.append(keep.tile([P, CHUNK], U32, name=f"codes{c}", align_bytes=64))
-            scale.append(keep.tile([P, CHUNK], U8, name=f"scale{c}", align_bytes=64))
+        codes = keep.tile([P, S], U32, name="codes", align_bytes=64)
+        scale = keep.tile([P, S], U8, name="scale", align_bytes=64)
+        for cols in spans(QUANT_WIDTHS):
+            h, r = divmod(cols.start, HALF)
             nc.vector.quantize_mx(
-                out=codes[c][:].bitcast(FP8X4),
-                scales=scale[c][:],
-                in_=picked[h][:, r : r + CHUNK, :].rearrange("p n j -> p (n j)"),
+                out=codes[:, cols].bitcast(FP8X4),
+                scales=scale[:, cols],
+                in_=picked[h][:, r : r + cols.stop - cols.start, :].rearrange("p n j -> p (n j)"),
             )
-        for h in range(2):
-            chunks = range(h * per_half, (h + 1) * per_half)
-            best = {}
-            for i in range(3):
-                for c in chunks:
-                    bank = psum.tile([P, CHUNK], F32, name="bank", tag="bank", bufs=8)
-                    nc.tensor.matmul_mx(
-                        out=bank[:],
-                        lhsT=w_codes[:, i * 2 * N : (i + 1) * 2 * N].bitcast(FP4X4),
-                        lhsT_scale=w_bytes[:, i * N : (i + 1) * N],
-                        rhs=codes[c][:].bitcast(FP8X4),
-                        rhs_scale=scale[c][:],
-                        start=True,
-                        stop=True,
-                    )
-                    result = keep.tile([P, CHUNK], F32, name=f"best{i}_{c}")
-                    if i == 0:
-                        nc.scalar.activation(result[:], bank[:], COPY)
-                    else:
-                        nc.vector.tensor_tensor(result[:], bank[:], best[c][:], MAX)
-                    best[c] = result
-            for c in chunks:
-                nc.sync.dma_start(out[:, c * CHUNK : (c + 1) * CHUNK], best[c][:])
+
+        chunks = spans(CHUNKS)
+        first = keep.tile([P, S], F32, name="first", tag="last_bf")
+        second = keep.tile([P, S], F32, name="second", tag="picked1", align_bytes=64)
+        third = keep.tile([P, S], F32, name="third")
+        best = (first, second, third)
+
+        def product(i, c):
+            cols = chunks[c]
+            width = CHUNKS[c]
+            bank = psum.tile([P, width], F32, name="bank", tag="bank", bufs=8)
+            nc.tensor.matmul_mx(
+                out=bank[:],
+                lhsT=w_codes[:, i * 2 * N : (i + 1) * 2 * N].bitcast(FP4X4),
+                lhsT_scale=w_bytes[:, i * N : (i + 1) * N],
+                rhs=codes[:, cols].bitcast(FP8X4),
+                rhs_scale=scale[:, cols],
+                start=True,
+                stop=True,
+            )
+            if i == 0:
+                nc.scalar.activation(first[:, cols], bank[:], COPY)
+            else:
+                nc.vector.tensor_tensor(best[i][:, cols], bank[:], best[i - 1][:, cols], MAX)
+
+        for c in range(len(CHUNKS) + 1):
+            if c < len(CHUNKS):
+                product(0, c)
+                product(1, c)
+            if c > 0:
+                product(2, c - 1)
+                nc.sync.dma_start(out[:, chunks[c - 1]], third[:, chunks[c - 1]])

@@ -19,17 +19,23 @@ MAX = mybir.AluOpType.max
 P = 128
 PACK = 4
 HALF = S // 2
+WEIGHTS = 3
+SCALE_ROWS = K // 32
+QUADRANTS = 4
+PSUM_BANKS = 8
+
 LAST_PIECES = ((1152, 1152), (1024, 0), (0, 512), (256, 0))
 QUANT_WIDTHS = (128, 128, 256, 256, 256)
-CHUNKS = (128, 256, 256, 256, 128)
+CHUNKS = (128, 384, 256, 128, 128)
+PASS_WIDTH = 256
 
 
 def spans(widths):
-    out, start = [], 0
+    result, start = [], 0
     for width in widths:
-        out.append(slice(start, start + width))
+        result.append(slice(start, start + width))
         start = start + width
-    return out
+    return result
 
 
 def tile_picked_maxout_max_e_kernel(tc, xT, w1_words, w1_scales, w2_words, w2_scales, w3_words, w3_scales, offs, out):
@@ -45,20 +51,20 @@ def tile_picked_maxout_max_e_kernel(tc, xT, w1_words, w1_scales, w2_words, w2_sc
         picked = [keep.tile([P, HALF, PACK], BF16, name=f"picked{h}", tag=f"picked{h}", align_bytes=64) for h in range(2)]
         half_offs = [offsets[:, h * (HALF // 16) : (h + 1) * (HALF // 16)] for h in range(2)]
 
-        w_codes = keep.tile([P, 3 * 2 * N], U8, name="w_codes", align_bytes=64)
-        w_bytes = keep.tile([P, 3 * N], U8, name="w_bytes", align_bytes=64)
-        staged = keep.tile([16, 3 * N], U8, name="staged", align_bytes=64)
+        w_codes = keep.tile([P, WEIGHTS * 2 * N], U8, name="w_codes", align_bytes=64)
+        w_bytes = keep.tile([P, WEIGHTS * N], U8, name="w_bytes", align_bytes=64)
+        staged = keep.tile([SCALE_ROWS, WEIGHTS * N], U8, name="staged", align_bytes=64)
         nc.vector.memset(w_bytes[:].bitcast(I32), 0)
 
         last = PACK - 1
         pieces = spans([a + b for a, b in LAST_PIECES])
         nc.sync.dma_start(planes[0][:], rows[:, 0, :])
         nc.sync.dma_start(offsets[:], offs)
-        for i, scales in enumerate((w1_scales, w2_scales, w3_scales)):
-            nc.sync.dma_start(staged[:, i * N : (i + 1) * N].bitcast(I32), scales[0].bitcast(I32))
+        for i, scale_rows in enumerate((w1_scales, w2_scales, w3_scales)):
+            nc.sync.dma_start(staged[:, i * N : (i + 1) * N].bitcast(I32), scale_rows[0].bitcast(I32))
         for j in range(1, last):
             nc.sync.dma_start(planes[j][:], rows[:, j, :])
-        for q in range(4):
+        for q in range(QUADRANTS):
             nc.sync.dma_start(w_bytes[32 * q : 32 * q + 4, :].bitcast(I32), staged[4 * q : 4 * q + 4, :].bitcast(I32))
         for cols in pieces:
             nc.sync.dma_start(planes[last][:, cols], rows[:, last, cols])
@@ -98,16 +104,18 @@ def tile_picked_maxout_max_e_kernel(tc, xT, w1_words, w1_scales, w2_words, w2_sc
         def product(i, c):
             cols = chunks[c]
             width = CHUNKS[c]
-            bank = psum.tile([P, width], F32, name="bank", tag="bank", bufs=8)
-            nc.tensor.matmul_mx(
-                out=bank[:],
-                lhsT=w_codes[:, i * 2 * N : (i + 1) * 2 * N].bitcast(FP4X4),
-                lhsT_scale=w_bytes[:, i * N : (i + 1) * N],
-                rhs=codes[:, cols].bitcast(FP8X4),
-                rhs_scale=scale[:, cols],
-                start=True,
-                stop=True,
-            )
+            bank = psum.tile([P, width], F32, name="bank", tag="bank", bufs=PSUM_BANKS)
+            for lo in range(0, width, PASS_WIDTH):
+                hi = min(lo + PASS_WIDTH, width)
+                nc.tensor.matmul_mx(
+                    out=bank[:, lo:hi],
+                    lhsT=w_codes[:, i * 2 * N : (i + 1) * 2 * N].bitcast(FP4X4),
+                    lhsT_scale=w_bytes[:, i * N : (i + 1) * N],
+                    rhs=codes[:, cols.start + lo : cols.start + hi].bitcast(FP8X4),
+                    rhs_scale=scale[:, cols.start + lo : cols.start + hi],
+                    start=True,
+                    stop=True,
+                )
             if i == 0:
                 nc.scalar.activation(first[:, cols], bank[:], COPY)
             else:

@@ -27,7 +27,8 @@ PSUM_BANKS = 8
 LAST_PIECES = ((1152, 1152), (1024, 0), (0, 512), (256, 0))
 QUANT_WIDTHS = (128, 128, 256, 256, 256)
 CHUNKS = (128, 384, 256, 128, 128)
-PASS_WIDTH = 256
+PASSES = {128: (128,), 256: (256,), 384: (128, 128, 128)}
+WARM_UP_WIDTHS = (512, 256)
 
 
 def spans(widths):
@@ -55,6 +56,7 @@ def tile_picked_maxout_max_e_kernel(tc, xT, w1_words, w1_scales, w2_words, w2_sc
         w_bytes = keep.tile([P, WEIGHTS * N], U8, name="w_bytes", align_bytes=64)
         staged = keep.tile([SCALE_ROWS, WEIGHTS * N], U8, name="staged", align_bytes=64)
         nc.vector.memset(w_bytes[:].bitcast(I32), 0)
+        nc.vector.memset(picked[0][:].rearrange("p n j -> p (n j)").bitcast(I32), 0)
 
         last = PACK - 1
         pieces = spans([a + b for a, b in LAST_PIECES])
@@ -71,9 +73,25 @@ def tile_picked_maxout_max_e_kernel(tc, xT, w1_words, w1_scales, w2_words, w2_sc
         for i, words in enumerate((w1_words, w2_words, w3_words)):
             nc.sync.dma_start(w_codes[:, i * 2 * N : (i + 1) * 2 * N].bitcast(I32), words[0].bitcast(I32))
 
+        warm_codes = keep.tile([P, HALF], U32, name="warm_codes", align_bytes=64)
+        warm_scale = keep.tile([P, HALF], U8, name="warm_scale", align_bytes=64)
         for j in range(last):
             for h in range(2):
                 nc.vector.tensor_copy(picked[h][:, :, j], planes[j][:].indirect(half_offs[h]))
+            if j == 0:
+                nc.vector.quantize_mx(out=warm_codes[:].bitcast(FP8X4), scales=warm_scale[:], in_=picked[0][:].rearrange("p n j -> p (n j)"))
+
+        for width in WARM_UP_WIDTHS:
+            unread = psum.tile([P, width], F32, name="bank", tag="bank", bufs=PSUM_BANKS)
+            nc.tensor.matmul_mx(
+                out=unread[:],
+                lhsT=w_codes[:, (WEIGHTS - 1) * 2 * N :].bitcast(FP4X4),
+                lhsT_scale=w_bytes[:, (WEIGHTS - 1) * N :],
+                rhs=warm_codes[:, :width].bitcast(FP8X4),
+                rhs_scale=warm_scale[:, :width],
+                start=True,
+                stop=True,
+            )
 
         for cols, (on_scalar, on_vector) in zip(pieces, LAST_PIECES):
             cut = cols.start + on_scalar
@@ -105,8 +123,8 @@ def tile_picked_maxout_max_e_kernel(tc, xT, w1_words, w1_scales, w2_words, w2_sc
             cols = chunks[c]
             width = CHUNKS[c]
             bank = psum.tile([P, width], F32, name="bank", tag="bank", bufs=PSUM_BANKS)
-            for lo in range(0, width, PASS_WIDTH):
-                hi = min(lo + PASS_WIDTH, width)
+            for part in spans(PASSES[width]):
+                lo, hi = part.start, part.stop
                 nc.tensor.matmul_mx(
                     out=bank[:, lo:hi],
                     lhsT=w_codes[:, i * 2 * N : (i + 1) * 2 * N].bitcast(FP4X4),

@@ -27,7 +27,7 @@ PSUM_BANKS = 8
 LAST_PIECES = ((1152, 1152), (1024, 0), (0, 512), (256, 0))
 QUANT_WIDTHS = (128, 128, 256, 256, 256)
 CHUNKS = (128, 384, 256, 128, 128)
-PASSES = {128: (128,), 256: (256,), 384: (128, 128, 128)}
+PASSES = ((128,), (128, 256), (256,), (256,), ())
 WARM_UP_WIDTHS = (512, 256)
 
 
@@ -118,12 +118,14 @@ def tile_picked_maxout_max_e_kernel(tc, xT, w1_words, w1_scales, w2_words, w2_sc
         second = keep.tile([P, S], F32, name="second", tag="picked1", align_bytes=64)
         third = keep.tile([P, S], F32, name="third")
         best = (first, second, third)
+        banks = {}
 
         def product(i, c):
             cols = chunks[c]
-            width = CHUNKS[c]
-            bank = psum.tile([P, width], F32, name="bank", tag="bank", bufs=PSUM_BANKS)
-            for part in spans(PASSES[width]):
+            if PASSES[c]:
+                banks[i] = (psum.tile([P, sum(PASSES[c])], F32, name="bank", tag="bank", bufs=PSUM_BANKS), cols.start)
+            bank, bank_start = banks[i]
+            for part in spans(PASSES[c]):
                 lo, hi = part.start, part.stop
                 nc.tensor.matmul_mx(
                     out=bank[:, lo:hi],
@@ -134,10 +136,11 @@ def tile_picked_maxout_max_e_kernel(tc, xT, w1_words, w1_scales, w2_words, w2_sc
                     start=True,
                     stop=True,
                 )
+            result = bank[:, cols.start - bank_start : cols.stop - bank_start]
             if i == 0:
-                nc.scalar.activation(first[:, cols], bank[:], COPY)
+                nc.scalar.activation(first[:, cols], result, COPY)
             else:
-                nc.vector.tensor_tensor(best[i][:, cols], bank[:], best[i - 1][:, cols], MAX)
+                nc.vector.tensor_tensor(best[i][:, cols], result, best[i - 1][:, cols], MAX)
 
         for c in range(len(CHUNKS) + 1):
             if c < len(CHUNKS):

@@ -26,8 +26,8 @@ PSUM_BANKS = 8
 
 LAST_PIECES = ((1152, 1152), (1024, 0), (0, 512), (256, 0))
 QUANT_WIDTHS = (128, 128, 256, 256, 256)
-CHUNKS = (128, 384, 256, 128, 128)
-PASSES = ((128,), (128, 256), (256,), (256,), ())
+CHUNKS = (256, 256, 256, 128, 128)
+PASSES = ((128, 128), (256,), (128, 128), (128,), (128,))
 WARM_UP_WIDTHS = (512, 256)
 
 

@@ -24,7 +24,7 @@ SCALE_ROWS = K // 32
 QUADRANTS = 4
 PSUM_BANKS = 8
 
-LAST_PIECES = ((1152, 1152), (1024, 0), (0, 512), (256, 0))
+LAST_PIECES = ((1536, 0), (768, 1024), (0, 512), (256, 0))
 QUANT_WIDTHS = (128, 128, 256, 256, 256)
 CHUNKS = (256, 256, 256, 128, 128)
 PASSES = ((128, 128), (256,), (128, 128), (128,), (128,))
@@ -115,7 +115,7 @@ def tile_picked_maxout_max_e_kernel(tc, xT, w1_words, w1_scales, w2_words, w2_sc
 
         chunks = spans(CHUNKS)
         first = keep.tile([P, S], F32, name="first", tag="last_bf")
-        second = keep.tile([P, S], F32, name="second", tag="picked1", align_bytes=64)
+        second = keep.tile([P, S], F32, name="second")
         third = keep.tile([P, S], F32, name="third")
         best = (first, second, third)
         banks = {}
@@ -142,10 +142,11 @@ def tile_picked_maxout_max_e_kernel(tc, xT, w1_words, w1_scales, w2_words, w2_sc
             else:
                 nc.vector.tensor_tensor(best[i][:, cols], result, best[i - 1][:, cols], MAX)
 
-        for c in range(len(CHUNKS) + 1):
+        for c in range(len(CHUNKS) + 2):
             if c < len(CHUNKS):
                 product(0, c)
+            if c >= 2:
+                product(2, c - 2)
+                nc.sync.dma_start(out[:, chunks[c - 2]], third[:, chunks[c - 2]])
+            if c < len(CHUNKS):
                 product(1, c)
-            if c > 0:
-                product(2, c - 1)
-                nc.sync.dma_start(out[:, chunks[c - 1]], third[:, chunks[c - 1]])

@@ -66,10 +66,10 @@ def tile_picked_maxout_max_e_kernel(tc, xT, w1_words, w1_scales, w2_words, w2_sc
             nc.sync.dma_start(staged[:, i * N : (i + 1) * N].bitcast(I32), scale_rows[0].bitcast(I32))
         for j in range(1, last):
             nc.sync.dma_start(planes[j][:], rows[:, j, :])
-        for q in range(QUADRANTS):
-            nc.sync.dma_start(w_bytes[32 * q : 32 * q + 4, :].bitcast(I32), staged[4 * q : 4 * q + 4, :].bitcast(I32))
         for cols in pieces:
             nc.sync.dma_start(planes[last][:, cols], rows[:, last, cols])
+        for q in range(QUADRANTS):
+            nc.sync.dma_start(w_bytes[32 * q : 32 * q + 4, :].bitcast(I32), staged[4 * q : 4 * q + 4, :].bitcast(I32))
         for i, words in enumerate((w1_words, w2_words, w3_words)):
             nc.sync.dma_start(w_codes[:, i * 2 * N : (i + 1) * 2 * N].bitcast(I32), words[0].bitcast(I32))
 

@@ -28,6 +28,7 @@ LAST_PIECES = ((1536, 0), (768, 1024), (0, 512), (256, 0))
 QUANT_WIDTHS = (128, 128, 256, 256, 256)
 CHUNKS = (256, 256, 256, 128, 128)
 PASSES = ((128, 128), (256,), (128, 128), (128,), (128,))
+FILL = 2
 WARM_UP_WIDTHS = (512, 256)
 
 
@@ -120,33 +121,38 @@ def tile_picked_maxout_max_e_kernel(tc, xT, w1_words, w1_scales, w2_words, w2_sc
         best = (first, second, third)
         banks = {}
 
-        def product(i, c):
-            cols = chunks[c]
-            if PASSES[c]:
-                banks[i] = (psum.tile([P, sum(PASSES[c])], F32, name="bank", tag="bank", bufs=PSUM_BANKS), cols.start)
-            bank, bank_start = banks[i]
+        def multiply(i, c):
+            bank = psum.tile([P, CHUNKS[c]], F32, name="bank", tag="bank", bufs=PSUM_BANKS)
+            banks[i, c] = bank
             for part in spans(PASSES[c]):
-                lo, hi = part.start, part.stop
+                cols = slice(chunks[c].start + part.start, chunks[c].start + part.stop)
                 nc.tensor.matmul_mx(
-                    out=bank[:, lo:hi],
+                    out=bank[:, part],
                     lhsT=w_codes[:, i * 2 * N : (i + 1) * 2 * N].bitcast(FP4X4),
                     lhsT_scale=w_bytes[:, i * N : (i + 1) * N],
-                    rhs=codes[:, cols.start + lo : cols.start + hi].bitcast(FP8X4),
-                    rhs_scale=scale[:, cols.start + lo : cols.start + hi],
+                    rhs=codes[:, cols].bitcast(FP8X4),
+                    rhs_scale=scale[:, cols],
                     start=True,
                     stop=True,
                 )
-            result = bank[:, cols.start - bank_start : cols.stop - bank_start]
-            if i == 0:
-                nc.scalar.activation(first[:, cols], result, COPY)
-            else:
-                nc.vector.tensor_tensor(best[i][:, cols], result, best[i - 1][:, cols], MAX)
 
-        for c in range(len(CHUNKS) + 2):
-            if c < len(CHUNKS):
-                product(0, c)
+        def compare(i, c):
+            nc.vector.tensor_tensor(best[i][:, chunks[c]], banks[i, c][:], best[i - 1][:, chunks[c]], MAX)
+
+        count = len(CHUNKS)
+        third_made = 0
+        for c in range(count + 2):
+            if c < count:
+                multiply(0, c)
+                nc.scalar.activation(first[:, chunks[c]], banks[0, c][:], COPY)
+                if c >= FILL:
+                    upto = c + 1 if c == count - 1 else c
+                    for d in range(third_made, upto):
+                        multiply(2, d)
+                    third_made = upto
+                multiply(1, c)
             if c >= 2:
-                product(2, c - 2)
+                compare(2, c - 2)
                 nc.sync.dma_start(out[:, chunks[c - 2]], third[:, chunks[c - 2]])
-            if c < len(CHUNKS):
-                product(1, c)
+            if c < count:
+                compare(1, c)

@@ -18,16 +18,17 @@ MAX = mybir.AluOpType.max
 
 P = 128
 PACK = 4
-HALF = S // 2
 WEIGHTS = 3
 SCALE_ROWS = K // 32
 QUADRANTS = 4
 PSUM_BANKS = 8
 
-LAST_PIECES = ((1536, 0), (768, 1024), (0, 512), (256, 0))
-QUANT_WIDTHS = (128, 128, 256, 256, 256)
+LAST_PIECES = ((1664, 0), (768, 896), (0, 512), (256, 0))
+GROUPS = (128, 320)
+WEAVES = (128, 128, 192)
+QUANT_WIDTHS = (128, 128, 128, 128, 256, 256)
 CHUNKS = (256, 256, 256, 128, 128)
-PASSES = ((128, 128), (256,), (128, 128), (128,), (128,))
+PASSES = ((128, 128), (128, 128), (256,), (128,), (128,))
 FILL = 2
 WARM_UP_WIDTHS = (512, 256)
 
@@ -50,14 +51,20 @@ def tile_picked_maxout_max_e_kernel(tc, xT, w1_words, w1_scales, w2_words, w2_sc
         offsets = keep.tile([P, S // 16], U16, name="offsets")
         planes = [keep.tile([P, T], F32, name=f"plane{j}") for j in range(PACK)]
         last_bf = keep.tile([P, T], BF16, name="last_bf", tag="last_bf")
-        picked = [keep.tile([P, HALF, PACK], BF16, name=f"picked{h}", tag=f"picked{h}", align_bytes=64) for h in range(2)]
-        half_offs = [offsets[:, h * (HALF // 16) : (h + 1) * (HALF // 16)] for h in range(2)]
+        picked = keep.tile([P, S, PACK], BF16, name="picked", align_bytes=64)
+        warm_width = max(WARM_UP_WIDTHS)
+
+        def listed(entries):
+            return offsets[:, entries.start // 16 : entries.stop // 16]
+
+        def flat(entries):
+            return picked[:, entries, :].rearrange("p n j -> p (n j)")
 
         w_codes = keep.tile([P, WEIGHTS * 2 * N], U8, name="w_codes", align_bytes=64)
         w_bytes = keep.tile([P, WEIGHTS * N], U8, name="w_bytes", align_bytes=64)
         staged = keep.tile([SCALE_ROWS, WEIGHTS * N], U8, name="staged", align_bytes=64)
         nc.vector.memset(w_bytes[:].bitcast(I32), 0)
-        nc.vector.memset(picked[0][:].rearrange("p n j -> p (n j)").bitcast(I32), 0)
+        nc.vector.memset(flat(slice(0, warm_width)).bitcast(I32), 0)
 
         last = PACK - 1
         pieces = spans([a + b for a, b in LAST_PIECES])
@@ -74,25 +81,27 @@ def tile_picked_maxout_max_e_kernel(tc, xT, w1_words, w1_scales, w2_words, w2_sc
         for i, words in enumerate((w1_words, w2_words, w3_words)):
             nc.sync.dma_start(w_codes[:, i * 2 * N : (i + 1) * 2 * N].bitcast(I32), words[0].bitcast(I32))
 
-        warm_codes = keep.tile([P, HALF], U32, name="warm_codes", align_bytes=64)
-        warm_scale = keep.tile([P, HALF], U8, name="warm_scale", align_bytes=64)
+        warm_codes = keep.tile([P, warm_width], U32, name="warm_codes", align_bytes=64)
+        warm_scale = keep.tile([P, warm_width], U8, name="warm_scale", align_bytes=64)
         for j in range(last):
-            for h in range(2):
-                nc.vector.tensor_copy(picked[h][:, :, j], planes[j][:].indirect(half_offs[h]))
+            nc.vector.tensor_copy(picked[:, :, j], planes[j][:].indirect(offsets[:]))
             if j == 0:
-                nc.vector.quantize_mx(out=warm_codes[:].bitcast(FP8X4), scales=warm_scale[:], in_=picked[0][:].rearrange("p n j -> p (n j)"))
+                nc.vector.quantize_mx(out=warm_codes[:].bitcast(FP8X4), scales=warm_scale[:], in_=flat(slice(0, warm_width)))
 
-        for width in WARM_UP_WIDTHS:
-            unread = psum.tile([P, width], F32, name="bank", tag="bank", bufs=PSUM_BANKS)
+        def pass_mx(bank, i, rhs, rhs_scale):
             nc.tensor.matmul_mx(
-                out=unread[:],
-                lhsT=w_codes[:, (WEIGHTS - 1) * 2 * N :].bitcast(FP4X4),
-                lhsT_scale=w_bytes[:, (WEIGHTS - 1) * N :],
-                rhs=warm_codes[:, :width].bitcast(FP8X4),
-                rhs_scale=warm_scale[:, :width],
+                out=bank,
+                lhsT=w_codes[:, i * 2 * N : (i + 1) * 2 * N].bitcast(FP4X4),
+                lhsT_scale=w_bytes[:, i * N : (i + 1) * N],
+                rhs=rhs.bitcast(FP8X4),
+                rhs_scale=rhs_scale,
                 start=True,
                 stop=True,
             )
+
+        for width in WARM_UP_WIDTHS:
+            unread = psum.tile([P, width], F32, name="bank", tag="bank", bufs=PSUM_BANKS)
+            pass_mx(unread[:], WEIGHTS - 1, warm_codes[:, :width], warm_scale[:, :width])
 
         for cols, (on_scalar, on_vector) in zip(pieces, LAST_PIECES):
             cut = cols.start + on_scalar
@@ -101,18 +110,24 @@ def tile_picked_maxout_max_e_kernel(tc, xT, w1_words, w1_scales, w2_words, w2_sc
             if on_vector:
                 nc.vector.tensor_copy(last_bf[:, cut : cols.stop], planes[last][:, cut : cols.stop])
 
-        nc.vector.tensor_copy(picked[0][:, :, last], planes[last][:].indirect(half_offs[0]))
-        nc.scalar.activation(picked[1][:, :, last], last_bf[:].indirect(half_offs[1]), COPY)
+        rest = slice(sum(GROUPS), S)
+        nc.scalar.activation(picked[:, rest, last], last_bf[:].indirect(listed(rest)), COPY)
 
         codes = keep.tile([P, S], U32, name="codes", align_bytes=64)
         scale = keep.tile([P, S], U8, name="scale", align_bytes=64)
-        for cols in spans(QUANT_WIDTHS):
-            h, r = divmod(cols.start, HALF)
-            nc.vector.quantize_mx(
-                out=codes[:, cols].bitcast(FP8X4),
-                scales=scale[:, cols],
-                in_=picked[h][:, r : r + cols.stop - cols.start, :].rearrange("p n j -> p (n j)"),
-            )
+        calls = spans(QUANT_WIDTHS)
+        quantised = 0
+        dense = keep.tile([P, sum(GROUPS)], BF16, name="dense")
+        for entries in spans(GROUPS):
+            nc.vector.tensor_copy(dense[:, entries], planes[last][:].indirect(listed(entries)))
+        for entries in spans(WEAVES):
+            nc.vector.tensor_copy(picked[:, entries, last], dense[:, entries])
+            while calls[quantised].stop <= entries.stop:
+                cols = calls[quantised]
+                nc.vector.quantize_mx(out=codes[:, cols].bitcast(FP8X4), scales=scale[:, cols], in_=flat(cols))
+                quantised = quantised + 1
+        for cols in calls[quantised:]:
+            nc.vector.quantize_mx(out=codes[:, cols].bitcast(FP8X4), scales=scale[:, cols], in_=flat(cols))
 
         chunks = spans(CHUNKS)
         first = keep.tile([P, S], F32, name="first", tag="last_bf")
@@ -126,15 +141,7 @@ def tile_picked_maxout_max_e_kernel(tc, xT, w1_words, w1_scales, w2_words, w2_sc
             banks[i, c] = bank
             for part in spans(PASSES[c]):
                 cols = slice(chunks[c].start + part.start, chunks[c].start + part.stop)
-                nc.tensor.matmul_mx(
-                    out=bank[:, part],
-                    lhsT=w_codes[:, i * 2 * N : (i + 1) * 2 * N].bitcast(FP4X4),
-                    lhsT_scale=w_bytes[:, i * N : (i + 1) * N],
-                    rhs=codes[:, cols].bitcast(FP8X4),
-                    rhs_scale=scale[:, cols],
-                    start=True,
-                    stop=True,
-                )
+                pass_mx(bank[:, part], i, codes[:, cols], scale[:, cols])
 
         def compare(i, c):
             nc.vector.tensor_tensor(best[i][:, chunks[c]], banks[i, c][:], best[i - 1][:, chunks[c]], MAX)

@@ -23,10 +23,10 @@ SCALE_ROWS = K // 32
 QUADRANTS = 4
 PSUM_BANKS = 8
 
-LAST_PIECES = ((1664, 0), (768, 896), (0, 512), (256, 0))
+LAST_PIECES = ((1664, 0), (768, 896), (0, 512), (128, 128))
 GROUPS = (128, 320)
 WEAVES = (128, 128, 192)
-QUANT_WIDTHS = (128, 128, 128, 128, 256, 256)
+QUANT_WIDTHS = (128, 128, 128, 64, 64, 256, 256)
 CHUNKS = (256, 256, 256, 128, 128)
 PASSES = ((128, 128), (128, 128), (256,), (128,), (128,))
 FILL = 2

@@ -24,17 +24,15 @@ QUADRANTS = 4
 PSUM_BANKS = 8
 
 LAST_PIECES = ((1664, 0), (768, 896), (0, 512), (128, 128))
-GROUPS = (128, 320)
-WEAVES = (128, 128, 192)
+GROUPS = (128, 128, 192)
 QUANT_WIDTHS = (128, 128, 128, 64, 64, 256, 256)
-CHUNKS = (256, 256, 256, 128, 128)
-PASSES = ((128, 128), (128, 128), (256,), (128,), (128,))
-FILL = 2
+CHUNKS = (128, 128, 256, 256, 256)
+NARROW = 128
 WARM_UP_WIDTHS = (512, 256)
 
 
-def spans(widths):
-    result, start = [], 0
+def spans(widths, start=0):
+    result = []
     for width in widths:
         result.append(slice(start, start + width))
         start = start + width
@@ -49,7 +47,7 @@ def tile_picked_maxout_max_e_kernel(tc, xT, w1_words, w1_scales, w2_words, w2_sc
         psum = ctx.enter_context(tc.psum_pool(name="psum", bufs=1))
 
         offsets = keep.tile([P, S // 16], U16, name="offsets")
-        planes = [keep.tile([P, T], F32, name=f"plane{j}") for j in range(PACK)]
+        planes = [keep.tile([P, T], F32, name=f"plane{j}", tag=f"plane{j}") for j in range(PACK)]
         last_bf = keep.tile([P, T], BF16, name="last_bf", tag="last_bf")
         picked = keep.tile([P, S, PACK], BF16, name="picked", align_bytes=64)
         warm_width = max(WARM_UP_WIDTHS)
@@ -74,11 +72,11 @@ def tile_picked_maxout_max_e_kernel(tc, xT, w1_words, w1_scales, w2_words, w2_sc
             nc.sync.dma_start(staged[:, i * N : (i + 1) * N].bitcast(I32), scale_rows[0].bitcast(I32))
         for j in range(1, last):
             nc.sync.dma_start(planes[j][:], rows[:, j, :])
-        for cols in pieces:
-            nc.sync.dma_start(planes[last][:, cols], rows[:, last, cols])
         for q in range(QUADRANTS):
             nc.sync.dma_start(w_bytes[32 * q : 32 * q + 4, :].bitcast(I32), staged[4 * q : 4 * q + 4, :].bitcast(I32))
-        for i, words in enumerate((w1_words, w2_words, w3_words)):
+        for cols in pieces:
+            nc.sync.dma_start(planes[last][:, cols], rows[:, last, cols])
+        for i, words in reversed(list(enumerate((w1_words, w2_words, w3_words)))):
             nc.sync.dma_start(w_codes[:, i * 2 * N : (i + 1) * 2 * N].bitcast(I32), words[0].bitcast(I32))
 
         warm_codes = keep.tile([P, warm_width], U32, name="warm_codes", align_bytes=64)
@@ -99,9 +97,9 @@ def tile_picked_maxout_max_e_kernel(tc, xT, w1_words, w1_scales, w2_words, w2_sc
                 stop=True,
             )
 
-        for width in WARM_UP_WIDTHS:
-            unread = psum.tile([P, width], F32, name="bank", tag="bank", bufs=PSUM_BANKS)
-            pass_mx(unread[:], WEIGHTS - 1, warm_codes[:, :width], warm_scale[:, :width])
+        for b, width in enumerate(WARM_UP_WIDTHS):
+            unread = psum.tile([P, width], F32, name="unread", tag=f"bank{len(CHUNKS) + b}")
+            pass_mx(unread[:], 0, warm_codes[:, :width], warm_scale[:, :width])
 
         for cols, (on_scalar, on_vector) in zip(pieces, LAST_PIECES):
             cut = cols.start + on_scalar
@@ -116,50 +114,75 @@ def tile_picked_maxout_max_e_kernel(tc, xT, w1_words, w1_scales, w2_words, w2_sc
         codes = keep.tile([P, S], U32, name="codes", align_bytes=64)
         scale = keep.tile([P, S], U8, name="scale", align_bytes=64)
         calls = spans(QUANT_WIDTHS)
-        quantised = 0
-        dense = keep.tile([P, sum(GROUPS)], BF16, name="dense")
-        for entries in spans(GROUPS):
-            nc.vector.tensor_copy(dense[:, entries], planes[last][:].indirect(listed(entries)))
-        for entries in spans(WEAVES):
-            nc.vector.tensor_copy(picked[:, entries, last], dense[:, entries])
-            while calls[quantised].stop <= entries.stop:
-                cols = calls[quantised]
-                nc.vector.quantize_mx(out=codes[:, cols].bitcast(FP8X4), scales=scale[:, cols], in_=flat(cols))
-                quantised = quantised + 1
-        for cols in calls[quantised:]:
+        groups = spans(GROUPS)
+
+        def quantise(cols):
             nc.vector.quantize_mx(out=codes[:, cols].bitcast(FP8X4), scales=scale[:, cols], in_=flat(cols))
 
+        dense = [keep.tile([P, GROUPS[g]], BF16, name=f"dense{g}", tag=f"dense{g}") for g in range(2)]
+        for g in range(2):
+            nc.vector.tensor_copy(dense[g][:], planes[last][:].indirect(listed(groups[g])))
+        nc.vector.tensor_copy(picked[:, groups[0], last], dense[0][:])
+        nc.vector.tensor_copy(picked[:, groups[1], last], dense[1][:])
+        quantise(calls[0])
+        late = keep.tile([P, GROUPS[2]], BF16, name="late", tag="dense0")
+        nc.vector.tensor_copy(late[:], planes[last][:].indirect(listed(groups[2])))
+        for part in spans((NARROW, GROUPS[2] - NARROW)):
+            entries = slice(groups[2].start + part.start, groups[2].start + part.stop)
+            nc.vector.tensor_copy(picked[:, entries, last], late[:, part])
+        for cols in calls[1:]:
+            quantise(cols)
+
         chunks = spans(CHUNKS)
+        count = len(CHUNKS)
         first = keep.tile([P, S], F32, name="first", tag="last_bf")
         second = keep.tile([P, S], F32, name="second")
         third = keep.tile([P, S], F32, name="third")
-        best = (first, second, third)
-        banks = {}
+        pair, lone = {}, {}
 
-        def multiply(i, c):
-            bank = psum.tile([P, CHUNKS[c]], F32, name="bank", tag="bank", bufs=PSUM_BANKS)
-            banks[i, c] = bank
-            for part in spans(PASSES[c]):
-                cols = slice(chunks[c].start + part.start, chunks[c].start + part.stop)
-                pass_mx(bank[:, part], i, codes[:, cols], scale[:, cols])
+        def multiply(bank, i, cols):
+            pass_mx(bank, i, codes[:, cols], scale[:, cols])
 
-        def compare(i, c):
-            nc.vector.tensor_tensor(best[i][:, chunks[c]], banks[i, c][:], best[i - 1][:, chunks[c]], MAX)
+        def first_two(c):
+            pair[c] = psum.tile([P, WEIGHTS if CHUNKS[c] == NARROW else 2, CHUNKS[c]], F32, name="pair", tag=f"bank{c}")
+            width = NARROW if chunks[c].start < S // 2 else CHUNKS[c]
+            for part in spans([width] * (CHUNKS[c] // width)):
+                for i in range(2):
+                    multiply(pair[c][:, i, part], i, slice(chunks[c].start + part.start, chunks[c].start + part.stop))
 
-        count = len(CHUNKS)
-        third_made = 0
-        for c in range(count + 2):
+        def last_one(c):
+            if CHUNKS[c] == NARROW:
+                lone[c] = pair[c][:, 2, :]
+            else:
+                bank = psum.tile([P, CHUNKS[c]], F32, name="lone", tag=f"bank{count + c - 2 if c < count - 1 else 0}")
+                lone[c] = bank[:]
+            for part in spans([NARROW] * (CHUNKS[c] // NARROW)):
+                multiply(lone[c][:, part], 2, slice(chunks[c].start + part.start, chunks[c].start + part.stop))
+
+        def compare_first(c):
+            nc.scalar.activation(first[:, chunks[c]], pair[c][:, 0, :], COPY)
+            nc.vector.tensor_tensor(second[:, chunks[c]], pair[c][:, 1, :], first[:, chunks[c]], MAX)
+
+        def compare_last(c, part):
+            cols = slice(chunks[c].start + part.start, chunks[c].start + part.stop)
+            nc.vector.tensor_tensor(third[:, cols], lone[c][:, part], second[:, cols], MAX)
+
+        for c in range(2):
+            first_two(c)
+            last_one(c)
+        for c in range(2):
+            compare_first(c)
+        for c in range(2):
+            compare_last(c, slice(0, NARROW))
+        nc.sync.dma_start(out[:, : 2 * NARROW], third[:, : 2 * NARROW])
+        for c in range(2, count + 1):
             if c < count:
-                multiply(0, c)
-                nc.scalar.activation(first[:, chunks[c]], banks[0, c][:], COPY)
-                if c >= FILL:
-                    upto = c + 1 if c == count - 1 else c
-                    for d in range(third_made, upto):
-                        multiply(2, d)
-                    third_made = upto
-                multiply(1, c)
-            if c >= 2:
-                compare(2, c - 2)
-                nc.sync.dma_start(out[:, chunks[c - 2]], third[:, chunks[c - 2]])
-            if c < count:
-                compare(1, c)
+                first_two(c)
+                compare_first(c)
+            if c > 2:
+                last_one(c - 1)
+                widths = [NARROW, NARROW] if c == count else [CHUNKS[c - 1]]
+                for part in spans(widths):
+                    compare_last(c - 1, part)
+                    cols = slice(chunks[c - 1].start + part.start, chunks[c - 1].start + part.stop)
+                    nc.sync.dma_start(out[:, cols], third[:, cols])

@@ -25,7 +25,6 @@ PSUM_BANKS = 8
 
 LAST_PIECES = ((1664, 0), (768, 896), (0, 512), (128, 128))
 GROUPS = (128, 128, 192)
-QUANT_WIDTHS = (128, 128, 128, 64, 64, 256, 256)
 CHUNKS = (128, 128, 256, 256, 256)
 NARROW = 128
 WARM_UP_WIDTHS = (512, 256)
@@ -72,10 +71,10 @@ def tile_picked_maxout_max_e_kernel(tc, xT, w1_words, w1_scales, w2_words, w2_sc
             nc.sync.dma_start(staged[:, i * N : (i + 1) * N].bitcast(I32), scale_rows[0].bitcast(I32))
         for j in range(1, last):
             nc.sync.dma_start(planes[j][:], rows[:, j, :])
-        for q in range(QUADRANTS):
-            nc.sync.dma_start(w_bytes[32 * q : 32 * q + 4, :].bitcast(I32), staged[4 * q : 4 * q + 4, :].bitcast(I32))
         for cols in pieces:
             nc.sync.dma_start(planes[last][:, cols], rows[:, last, cols])
+        for q in range(QUADRANTS):
+            nc.sync.dma_start(w_bytes[32 * q : 32 * q + 4, :].bitcast(I32), staged[4 * q : 4 * q + 4, :].bitcast(I32))
         for i, words in reversed(list(enumerate((w1_words, w2_words, w3_words)))):
             nc.sync.dma_start(w_codes[:, i * 2 * N : (i + 1) * 2 * N].bitcast(I32), words[0].bitcast(I32))
 
@@ -108,13 +107,13 @@ def tile_picked_maxout_max_e_kernel(tc, xT, w1_words, w1_scales, w2_words, w2_sc
             if on_vector:
                 nc.vector.tensor_copy(last_bf[:, cut : cols.stop], planes[last][:, cut : cols.stop])
 
-        rest = slice(sum(GROUPS), S)
+        rest = slice(sum(GROUPS[:2]), S - GROUPS[2])
         nc.scalar.activation(picked[:, rest, last], last_bf[:].indirect(listed(rest)), COPY)
 
         codes = keep.tile([P, S], U32, name="codes", align_bytes=64)
         scale = keep.tile([P, S], U8, name="scale", align_bytes=64)
-        calls = spans(QUANT_WIDTHS)
-        groups = spans(GROUPS)
+        calls = spans(CHUNKS)
+        groups = spans(GROUPS[:2]) + [slice(rest.stop, S)]
 
         def quantise(cols):
             nc.vector.quantize_mx(out=codes[:, cols].bitcast(FP8X4), scales=scale[:, cols], in_=flat(cols))
@@ -127,10 +126,9 @@ def tile_picked_maxout_max_e_kernel(tc, xT, w1_words, w1_scales, w2_words, w2_sc
         quantise(calls[0])
         late = keep.tile([P, GROUPS[2]], BF16, name="late", tag="dense0")
         nc.vector.tensor_copy(late[:], planes[last][:].indirect(listed(groups[2])))
-        for part in spans((NARROW, GROUPS[2] - NARROW)):
-            entries = slice(groups[2].start + part.start, groups[2].start + part.stop)
-            nc.vector.tensor_copy(picked[:, entries, last], late[:, part])
-        for cols in calls[1:]:
+        quantise(calls[1])
+        nc.vector.tensor_copy(picked[:, groups[2], last], late[:])
+        for cols in calls[2:]:
             quantise(cols)
 
         chunks = spans(CHUNKS)

@@ -25,7 +25,8 @@ PSUM_BANKS = 8
 
 LAST_PIECES = ((1664, 0), (768, 896), (0, 512), (128, 128))
 GROUPS = (128, 128, 192)
-CHUNKS = (128, 128, 256, 256, 256)
+QUANT_WIDTHS = (128, 128, 256, 256, 256)
+CHUNKS = (128, 128, 256, 256, 128, 128)
 NARROW = 128
 WARM_UP_WIDTHS = (512, 256)
 
@@ -71,10 +72,10 @@ def tile_picked_maxout_max_e_kernel(tc, xT, w1_words, w1_scales, w2_words, w2_sc
             nc.sync.dma_start(staged[:, i * N : (i + 1) * N].bitcast(I32), scale_rows[0].bitcast(I32))
         for j in range(1, last):
             nc.sync.dma_start(planes[j][:], rows[:, j, :])
-        for cols in pieces:
-            nc.sync.dma_start(planes[last][:, cols], rows[:, last, cols])
         for q in range(QUADRANTS):
             nc.sync.dma_start(w_bytes[32 * q : 32 * q + 4, :].bitcast(I32), staged[4 * q : 4 * q + 4, :].bitcast(I32))
+        for cols in pieces:
+            nc.sync.dma_start(planes[last][:, cols], rows[:, last, cols])
         for i, words in reversed(list(enumerate((w1_words, w2_words, w3_words)))):
             nc.sync.dma_start(w_codes[:, i * 2 * N : (i + 1) * 2 * N].bitcast(I32), words[0].bitcast(I32))
 
@@ -112,7 +113,7 @@ def tile_picked_maxout_max_e_kernel(tc, xT, w1_words, w1_scales, w2_words, w2_sc
 
         codes = keep.tile([P, S], U32, name="codes", align_bytes=64)
         scale = keep.tile([P, S], U8, name="scale", align_bytes=64)
-        calls = spans(CHUNKS)
+        calls = spans(QUANT_WIDTHS)
         groups = spans(GROUPS[:2]) + [slice(rest.stop, S)]
 
         def quantise(cols):
@@ -136,51 +137,41 @@ def tile_picked_maxout_max_e_kernel(tc, xT, w1_words, w1_scales, w2_words, w2_sc
         first = keep.tile([P, S], F32, name="first", tag="last_bf")
         second = keep.tile([P, S], F32, name="second")
         third = keep.tile([P, S], F32, name="third")
-        pair, lone = {}, {}
+        product = {}
 
-        def multiply(bank, i, cols):
-            pass_mx(bank, i, codes[:, cols], scale[:, cols])
-
-        def first_two(c):
-            pair[c] = psum.tile([P, WEIGHTS if CHUNKS[c] == NARROW else 2, CHUNKS[c]], F32, name="pair", tag=f"bank{c}")
-            width = NARROW if chunks[c].start < S // 2 else CHUNKS[c]
+        def multiply(i, c, width):
             for part in spans([width] * (CHUNKS[c] // width)):
-                for i in range(2):
-                    multiply(pair[c][:, i, part], i, slice(chunks[c].start + part.start, chunks[c].start + part.stop))
+                cols = slice(chunks[c].start + part.start, chunks[c].start + part.stop)
+                pass_mx(product[i, c][:, part], i, codes[:, cols], scale[:, cols])
 
-        def last_one(c):
-            if CHUNKS[c] == NARROW:
-                lone[c] = pair[c][:, 2, :]
-            else:
-                bank = psum.tile([P, CHUNKS[c]], F32, name="lone", tag=f"bank{count + c - 2 if c < count - 1 else 0}")
-                lone[c] = bank[:]
-            for part in spans([NARROW] * (CHUNKS[c] // NARROW)):
-                multiply(lone[c][:, part], 2, slice(chunks[c].start + part.start, chunks[c].start + part.stop))
+        wide = [c for c in range(count) if CHUNKS[c] > NARROW]
+        for c in range(count):
+            together = 2 if c in wide else WEIGHTS
+            bank = psum.tile([P, together, CHUNKS[c]], F32, name="bank", tag=f"bank{c}")
+            for i in range(together):
+                product[i, c] = bank[:, i, :]
+                multiply(i, c, CHUNKS[c])
+            if c == wide[-1]:
+                for b, d in enumerate(wide):
+                    lone = psum.tile([P, CHUNKS[d]], F32, name="lone", tag=f"bank{count + b}")
+                    product[2, d] = lone[:]
+                    multiply(2, d, NARROW)
 
         def compare_first(c):
-            nc.scalar.activation(first[:, chunks[c]], pair[c][:, 0, :], COPY)
-            nc.vector.tensor_tensor(second[:, chunks[c]], pair[c][:, 1, :], first[:, chunks[c]], MAX)
+            nc.scalar.activation(first[:, chunks[c]], product[0, c], COPY)
+            nc.vector.tensor_tensor(second[:, chunks[c]], product[1, c], first[:, chunks[c]], MAX)
 
-        def compare_last(c, part):
-            cols = slice(chunks[c].start + part.start, chunks[c].start + part.stop)
-            nc.vector.tensor_tensor(third[:, cols], lone[c][:, part], second[:, cols], MAX)
+        def compare_last(c):
+            nc.vector.tensor_tensor(third[:, chunks[c]], product[2, c], second[:, chunks[c]], MAX)
 
-        for c in range(2):
-            first_two(c)
-            last_one(c)
         for c in range(2):
             compare_first(c)
         for c in range(2):
-            compare_last(c, slice(0, NARROW))
-        nc.sync.dma_start(out[:, : 2 * NARROW], third[:, : 2 * NARROW])
+            compare_last(c)
+        nc.sync.dma_start(out[:, : chunks[1].stop], third[:, : chunks[1].stop])
         for c in range(2, count + 1):
             if c < count:
-                first_two(c)
                 compare_first(c)
             if c > 2:
-                last_one(c - 1)
-                widths = [NARROW, NARROW] if c == count else [CHUNKS[c - 1]]
-                for part in spans(widths):
-                    compare_last(c - 1, part)
-                    cols = slice(chunks[c - 1].start + part.start, chunks[c - 1].start + part.stop)
-                    nc.sync.dma_start(out[:, cols], third[:, cols])
+                compare_last(c - 1)
+                nc.sync.dma_start(out[:, chunks[c - 1]], third[:, chunks[c - 1]])

@@ -24,7 +24,7 @@ QUADRANTS = 4
 PSUM_BANKS = 8
 
 LAST_PIECES = ((1664, 0), (768, 896), (0, 512), (128, 128))
-GROUPS = (128, 128, 192)
+GROUPS = (128, 128, 224)
 QUANT_WIDTHS = (128, 128, 256, 256, 256)
 CHUNKS = (128, 128, 256, 256, 128, 128)
 NARROW = 128
@@ -72,12 +72,22 @@ def tile_picked_maxout_max_e_kernel(tc, xT, w1_words, w1_scales, w2_words, w2_sc
             nc.sync.dma_start(staged[:, i * N : (i + 1) * N].bitcast(I32), scale_rows[0].bitcast(I32))
         for j in range(1, last):
             nc.sync.dma_start(planes[j][:], rows[:, j, :])
-        for q in range(QUADRANTS):
-            nc.sync.dma_start(w_bytes[32 * q : 32 * q + 4, :].bitcast(I32), staged[4 * q : 4 * q + 4, :].bitcast(I32))
         for cols in pieces:
             nc.sync.dma_start(planes[last][:, cols], rows[:, last, cols])
-        for i, words in reversed(list(enumerate((w1_words, w2_words, w3_words)))):
+
+        def load_codes(i):
+            words = (w1_words, w2_words, w3_words)[i]
             nc.sync.dma_start(w_codes[:, i * 2 * N : (i + 1) * 2 * N].bitcast(I32), words[0].bitcast(I32))
+
+        def move_scales(q):
+            nc.sync.dma_start(w_bytes[32 * q : 32 * q + 4, :].bitcast(I32), staged[4 * q : 4 * q + 4, :].bitcast(I32))
+
+        for i in range(WEIGHTS - 1):
+            load_codes(i)
+        for q in range(QUADRANTS - 1):
+            move_scales(q)
+        load_codes(WEIGHTS - 1)
+        move_scales(QUADRANTS - 1)
 
         warm_codes = keep.tile([P, warm_width], U32, name="warm_codes", align_bytes=64)
         warm_scale = keep.tile([P, warm_width], U8, name="warm_scale", align_bytes=64)
@@ -86,11 +96,11 @@ def tile_picked_maxout_max_e_kernel(tc, xT, w1_words, w1_scales, w2_words, w2_sc
             if j == 0:
                 nc.vector.quantize_mx(out=warm_codes[:].bitcast(FP8X4), scales=warm_scale[:], in_=flat(slice(0, warm_width)))
 
-        def pass_mx(bank, i, rhs, rhs_scale):
+        def pass_mx(bank, i, lhs_scale, rhs, rhs_scale):
             nc.tensor.matmul_mx(
                 out=bank,
                 lhsT=w_codes[:, i * 2 * N : (i + 1) * 2 * N].bitcast(FP4X4),
-                lhsT_scale=w_bytes[:, i * N : (i + 1) * N],
+                lhsT_scale=lhs_scale,
                 rhs=rhs.bitcast(FP8X4),
                 rhs_scale=rhs_scale,
                 start=True,
@@ -99,7 +109,7 @@ def tile_picked_maxout_max_e_kernel(tc, xT, w1_words, w1_scales, w2_words, w2_sc
 
         for b, width in enumerate(WARM_UP_WIDTHS):
             unread = psum.tile([P, width], F32, name="unread", tag=f"bank{len(CHUNKS) + b}")
-            pass_mx(unread[:], 0, warm_codes[:, :width], warm_scale[:, :width])
+            pass_mx(unread[:], WEIGHTS - 1, warm_scale[:, :N], warm_codes[:, :width], warm_scale[:, :width])
 
         for cols, (on_scalar, on_vector) in zip(pieces, LAST_PIECES):
             cut = cols.start + on_scalar
@@ -142,7 +152,7 @@ def tile_picked_maxout_max_e_kernel(tc, xT, w1_words, w1_scales, w2_words, w2_sc
         def multiply(i, c, width):
             for part in spans([width] * (CHUNKS[c] // width)):
                 cols = slice(chunks[c].start + part.start, chunks[c].start + part.stop)
-                pass_mx(product[i, c][:, part], i, codes[:, cols], scale[:, cols])
+                pass_mx(product[i, c][:, part], i, w_bytes[:, i * N : (i + 1) * N], codes[:, cols], scale[:, cols])
 
         wide = [c for c in range(count) if CHUNKS[c] > NARROW]
         for c in range(count):

@@ -24,7 +24,7 @@ QUADRANTS = 4
 PSUM_BANKS = 8
 
 LAST_PIECES = ((1664, 0), (768, 896), (0, 512), (128, 128))
-GROUPS = (128, 128, 224)
+GROUP = 128
 QUANT_WIDTHS = (128, 128, 256, 256, 256)
 CHUNKS = (128, 128, 256, 256, 128, 128)
 NARROW = 128
@@ -37,6 +37,10 @@ def spans(widths, start=0):
         result.append(slice(start, start + width))
         start = start + width
     return result
+
+
+def swapped(slices):
+    return slices[:2] + [slices[3], slices[2]] + slices[4:]
 
 
 def tile_picked_maxout_max_e_kernel(tc, xT, w1_words, w1_scales, w2_words, w2_scales, w3_words, w3_scales, offs, out):
@@ -118,31 +122,35 @@ def tile_picked_maxout_max_e_kernel(tc, xT, w1_words, w1_scales, w2_words, w2_sc
             if on_vector:
                 nc.vector.tensor_copy(last_bf[:, cut : cols.stop], planes[last][:, cut : cols.stop])
 
-        rest = slice(sum(GROUPS[:2]), S - GROUPS[2])
+        early = spans([GROUP] * 2)
+        late = [slice(2 * GROUP, 3 * GROUP), slice(S - GROUP, S)]
+        rest = slice(late[0].stop, late[1].start)
         nc.scalar.activation(picked[:, rest, last], last_bf[:].indirect(listed(rest)), COPY)
 
         codes = keep.tile([P, S], U32, name="codes", align_bytes=64)
         scale = keep.tile([P, S], U8, name="scale", align_bytes=64)
-        calls = spans(QUANT_WIDTHS)
-        groups = spans(GROUPS[:2]) + [slice(rest.stop, S)]
+        calls = swapped(spans(QUANT_WIDTHS))
 
         def quantise(cols):
             nc.vector.quantize_mx(out=codes[:, cols].bitcast(FP8X4), scales=scale[:, cols], in_=flat(cols))
 
-        dense = [keep.tile([P, GROUPS[g]], BF16, name=f"dense{g}", tag=f"dense{g}") for g in range(2)]
-        for g in range(2):
-            nc.vector.tensor_copy(dense[g][:], planes[last][:].indirect(listed(groups[g])))
-        nc.vector.tensor_copy(picked[:, groups[0], last], dense[0][:])
-        nc.vector.tensor_copy(picked[:, groups[1], last], dense[1][:])
-        quantise(calls[0])
-        late = keep.tile([P, GROUPS[2]], BF16, name="late", tag="dense0")
-        nc.vector.tensor_copy(late[:], planes[last][:].indirect(listed(groups[2])))
-        quantise(calls[1])
-        nc.vector.tensor_copy(picked[:, groups[2], last], late[:])
+        def gather(entries, buffer):
+            dense = keep.tile([P, GROUP], BF16, name="dense", tag=f"dense{buffer}")
+            nc.vector.tensor_copy(dense[:], planes[last][:].indirect(listed(entries)))
+            return dense
+
+        dense = [gather(entries, g) for g, entries in enumerate(early)]
+        for g, entries in enumerate(early):
+            nc.vector.tensor_copy(picked[:, entries, last], dense[g][:])
+        for g, entries in enumerate(late):
+            quantise(calls[g])
+            dense[g] = gather(entries, g)
+        nc.vector.tensor_copy(picked[:, late[0], last], dense[0][:])
+        nc.scalar.activation(picked[:, late[1], last], dense[1][:], COPY)
         for cols in calls[2:]:
             quantise(cols)
 
-        chunks = spans(CHUNKS)
+        chunks = swapped(spans(CHUNKS))
         count = len(CHUNKS)
         first = keep.tile([P, S], F32, name="first", tag="last_bf")
         second = keep.tile([P, S], F32, name="second")

@@ -21,14 +21,8 @@ PACK = 4
 WEIGHTS = 3
 SCALE_ROWS = K // 32
 QUADRANTS = 4
-PSUM_BANKS = 8
-
-LAST_PIECES = ((1664, 0), (768, 896), (0, 512), (128, 128))
 GROUP = 128
-QUANT_WIDTHS = (128, 128, 256, 256, 256)
 CHUNKS = (128, 128, 256, 256, 128, 128)
-NARROW = 128
-WARM_UP_WIDTHS = (512, 256)
 
 
 def spans(widths, start=0):
@@ -37,10 +31,6 @@ def spans(widths, start=0):
         result.append(slice(start, start + width))
         start = start + width
     return result
-
-
-def swapped(slices):
-    return slices[:2] + [slices[3], slices[2]] + slices[4:]
 
 
 def tile_picked_maxout_max_e_kernel(tc, xT, w1_words, w1_scales, w2_words, w2_scales, w3_words, w3_scales, offs, out):
@@ -52,9 +42,7 @@ def tile_picked_maxout_max_e_kernel(tc, xT, w1_words, w1_scales, w2_words, w2_sc
 
         offsets = keep.tile([P, S // 16], U16, name="offsets")
         planes = [keep.tile([P, T], F32, name=f"plane{j}", tag=f"plane{j}") for j in range(PACK)]
-        last_bf = keep.tile([P, T], BF16, name="last_bf", tag="last_bf")
         picked = keep.tile([P, S, PACK], BF16, name="picked", align_bytes=64)
-        warm_width = max(WARM_UP_WIDTHS)
 
         def listed(entries):
             return offsets[:, entries.start // 16 : entries.stop // 16]
@@ -66,114 +54,83 @@ def tile_picked_maxout_max_e_kernel(tc, xT, w1_words, w1_scales, w2_words, w2_sc
         w_bytes = keep.tile([P, WEIGHTS * N], U8, name="w_bytes", align_bytes=64)
         staged = keep.tile([SCALE_ROWS, WEIGHTS * N], U8, name="staged", align_bytes=64)
         nc.vector.memset(w_bytes[:].bitcast(I32), 0)
-        nc.vector.memset(flat(slice(0, warm_width)).bitcast(I32), 0)
 
         last = PACK - 1
-        pieces = spans([a + b for a, b in LAST_PIECES])
         nc.sync.dma_start(planes[0][:], rows[:, 0, :])
         nc.sync.dma_start(offsets[:], offs)
         for i, scale_rows in enumerate((w1_scales, w2_scales, w3_scales)):
             nc.sync.dma_start(staged[:, i * N : (i + 1) * N].bitcast(I32), scale_rows[0].bitcast(I32))
-        for j in range(1, last):
+        for j in range(1, PACK):
             nc.sync.dma_start(planes[j][:], rows[:, j, :])
-        for cols in pieces:
-            nc.sync.dma_start(planes[last][:, cols], rows[:, last, cols])
-
-        def load_codes(i):
-            words = (w1_words, w2_words, w3_words)[i]
+        for i, words in enumerate((w1_words, w2_words, w3_words)):
             nc.sync.dma_start(w_codes[:, i * 2 * N : (i + 1) * 2 * N].bitcast(I32), words[0].bitcast(I32))
-
-        def move_scales(q):
+        for q in range(QUADRANTS):
             nc.sync.dma_start(w_bytes[32 * q : 32 * q + 4, :].bitcast(I32), staged[4 * q : 4 * q + 4, :].bitcast(I32))
-
-        for i in range(WEIGHTS - 1):
-            load_codes(i)
-        for q in range(QUADRANTS - 1):
-            move_scales(q)
-        load_codes(WEIGHTS - 1)
-        move_scales(QUADRANTS - 1)
-
-        warm_codes = keep.tile([P, warm_width], U32, name="warm_codes", align_bytes=64)
-        warm_scale = keep.tile([P, warm_width], U8, name="warm_scale", align_bytes=64)
-        for j in range(last):
-            nc.vector.tensor_copy(picked[:, :, j], planes[j][:].indirect(offsets[:]))
-            if j == 0:
-                nc.vector.quantize_mx(out=warm_codes[:].bitcast(FP8X4), scales=warm_scale[:], in_=flat(slice(0, warm_width)))
-
-        def pass_mx(bank, i, lhs_scale, rhs, rhs_scale):
-            nc.tensor.matmul_mx(
-                out=bank,
-                lhsT=w_codes[:, i * 2 * N : (i + 1) * 2 * N].bitcast(FP4X4),
-                lhsT_scale=lhs_scale,
-                rhs=rhs.bitcast(FP8X4),
-                rhs_scale=rhs_scale,
-                start=True,
-                stop=True,
-            )
-
-        for b, width in enumerate(WARM_UP_WIDTHS):
-            unread = psum.tile([P, width], F32, name="unread", tag=f"bank{len(CHUNKS) + b}")
-            pass_mx(unread[:], WEIGHTS - 1, warm_scale[:, :N], warm_codes[:, :width], warm_scale[:, :width])
-
-        for cols, (on_scalar, on_vector) in zip(pieces, LAST_PIECES):
-            cut = cols.start + on_scalar
-            if on_scalar:
-                nc.scalar.activation(last_bf[:, cols.start : cut], planes[last][:, cols.start : cut], COPY)
-            if on_vector:
-                nc.vector.tensor_copy(last_bf[:, cut : cols.stop], planes[last][:, cut : cols.stop])
-
-        early = spans([GROUP] * 2)
-        late = [slice(2 * GROUP, 3 * GROUP), slice(S - GROUP, S)]
-        rest = slice(late[0].stop, late[1].start)
-        nc.scalar.activation(picked[:, rest, last], last_bf[:].indirect(listed(rest)), COPY)
 
         codes = keep.tile([P, S], U32, name="codes", align_bytes=64)
         scale = keep.tile([P, S], U8, name="scale", align_bytes=64)
-        calls = swapped(spans(QUANT_WIDTHS))
+        groups = spans([GROUP] * (S // GROUP))
+        pairs = spans([2 * GROUP] * (S // (2 * GROUP)))
 
         def quantise(cols):
             nc.vector.quantize_mx(out=codes[:, cols].bitcast(FP8X4), scales=scale[:, cols], in_=flat(cols))
 
-        def gather(entries, buffer):
-            dense = keep.tile([P, GROUP], BF16, name="dense", tag=f"dense{buffer}")
-            nc.vector.tensor_copy(dense[:], planes[last][:].indirect(listed(entries)))
-            return dense
+        def scalar_share(j):
+            own = keep.tile([P, 2 * GROUP], BF16, name="own", tag="own")
+            nc.scalar.activation(own[:], planes[j][:].indirect(listed(pairs[3])), COPY)
+            nc.scalar.activation(picked[:, pairs[3], j], own[:], COPY)
 
-        dense = [gather(entries, g) for g, entries in enumerate(early)]
-        for g, entries in enumerate(early):
-            nc.vector.tensor_copy(picked[:, entries, last], dense[g][:])
-        for g, entries in enumerate(late):
-            quantise(calls[g])
-            dense[g] = gather(entries, g)
-        nc.vector.tensor_copy(picked[:, late[0], last], dense[0][:])
-        nc.scalar.activation(picked[:, late[1], last], dense[1][:], COPY)
-        for cols in calls[2:]:
-            quantise(cols)
+        stepped = slice(0, pairs[3].start)
+        for j in range(last):
+            nc.vector.tensor_copy(picked[:, stepped, j], planes[j][:].indirect(listed(stepped)))
+            scalar_share(j)
 
-        chunks = swapped(spans(CHUNKS))
+        dense = [keep.tile([P, 2 * GROUP], BF16, name="dense", tag=f"dense{d}") for d in range(3)]
+        for g in range(2):
+            nc.vector.tensor_copy(dense[0][:, groups[g]], planes[last][:].indirect(listed(groups[g])))
+        for d in (1, 2):
+            nc.scalar.activation(dense[d][:], planes[last][:].indirect(listed(pairs[d])), COPY)
+
+        def weave(g):
+            nc.vector.tensor_copy(picked[:, groups[g], last], dense[g // 2][:, groups[g % 2]])
+
+        weave(0)
+        for g in range(1, 6):
+            weave(g)
+            quantise(groups[g - 1])
+        scalar_share(last)
+        quantise(groups[5])
+        quantise(pairs[3])
+
+        chunks = spans(CHUNKS)
         count = len(CHUNKS)
-        first = keep.tile([P, S], F32, name="first", tag="last_bf")
+        first = keep.tile([P, S], F32, name="first")
         second = keep.tile([P, S], F32, name="second")
         third = keep.tile([P, S], F32, name="third")
         product = {}
-
-        def multiply(i, c, width):
-            for part in spans([width] * (CHUNKS[c] // width)):
-                cols = slice(chunks[c].start + part.start, chunks[c].start + part.stop)
-                pass_mx(product[i, c][:, part], i, w_bytes[:, i * N : (i + 1) * N], codes[:, cols], scale[:, cols])
-
-        wide = [c for c in range(count) if CHUNKS[c] > NARROW]
+        spare = count
         for c in range(count):
-            together = 2 if c in wide else WEIGHTS
+            wide = CHUNKS[c] > GROUP
+            together = 2 if wide else WEIGHTS
             bank = psum.tile([P, together, CHUNKS[c]], F32, name="bank", tag=f"bank{c}")
             for i in range(together):
                 product[i, c] = bank[:, i, :]
-                multiply(i, c, CHUNKS[c])
-            if c == wide[-1]:
-                for b, d in enumerate(wide):
-                    lone = psum.tile([P, CHUNKS[d]], F32, name="lone", tag=f"bank{count + b}")
-                    product[2, d] = lone[:]
-                    multiply(2, d, NARROW)
+            if wide:
+                lone = psum.tile([P, CHUNKS[c]], F32, name="lone", tag=f"bank{spare}")
+                spare = spare + 1
+                product[2, c] = lone[:]
+            for part in spans([GROUP] * (CHUNKS[c] // GROUP)):
+                cols = slice(chunks[c].start + part.start, chunks[c].start + part.stop)
+                for i in range(WEIGHTS):
+                    nc.tensor.matmul_mx(
+                        out=product[i, c][:, part],
+                        lhsT=w_codes[:, i * 2 * N : (i + 1) * 2 * N].bitcast(FP4X4),
+                        lhsT_scale=w_bytes[:, i * N : (i + 1) * N],
+                        rhs=codes[:, cols].bitcast(FP8X4),
+                        rhs_scale=scale[:, cols],
+                        start=True,
+                        stop=True,
+                    )
 
         def compare_first(c):
             nc.scalar.activation(first[:, chunks[c]], product[0, c], COPY)

@@ -22,7 +22,6 @@ WEIGHTS = 3
 SCALE_ROWS = K // 32
 QUADRANTS = 4
 GROUP = 128
-CHUNKS = (128, 128, 256, 256, 128, 128)
 
 
 def spans(widths, start=0):
@@ -70,83 +69,66 @@ def tile_picked_maxout_max_e_kernel(tc, xT, w1_words, w1_scales, w2_words, w2_sc
         codes = keep.tile([P, S], U32, name="codes", align_bytes=64)
         scale = keep.tile([P, S], U8, name="scale", align_bytes=64)
         groups = spans([GROUP] * (S // GROUP))
-        pairs = spans([2 * GROUP] * (S // (2 * GROUP)))
 
         def quantise(cols):
             nc.vector.quantize_mx(out=codes[:, cols].bitcast(FP8X4), scales=scale[:, cols], in_=flat(cols))
 
-        def scalar_share(j):
-            own = keep.tile([P, 2 * GROUP], BF16, name="own", tag="own")
-            nc.scalar.activation(own[:], planes[j][:].indirect(listed(pairs[3])), COPY)
-            nc.scalar.activation(picked[:, pairs[3], j], own[:], COPY)
+        count = len(groups)
+        own = groups[count - 1]
+        stepped = slice(0, own.start)
 
-        stepped = slice(0, pairs[3].start)
+        def dense_tile(g):
+            return keep.tile([P, GROUP], BF16, name="dense", tag=f"dense{g}")
+
         for j in range(last):
             nc.vector.tensor_copy(picked[:, stepped, j], planes[j][:].indirect(listed(stepped)))
-            scalar_share(j)
+            early = dense_tile(count)
+            nc.scalar.activation(early[:], planes[j][:].indirect(listed(own)), COPY)
+            nc.scalar.activation(picked[:, own, j], early[:], COPY)
 
-        dense = [keep.tile([P, 2 * GROUP], BF16, name="dense", tag=f"dense{d}") for d in range(3)]
-        for g in range(2):
-            nc.vector.tensor_copy(dense[0][:, groups[g]], planes[last][:].indirect(listed(groups[g])))
-        for d in (1, 2):
-            nc.scalar.activation(dense[d][:], planes[last][:].indirect(listed(pairs[d])), COPY)
+        dense = [dense_tile(g) for g in range(count)]
+        for g in (0, count - 1):
+            nc.vector.tensor_copy(dense[g][:], planes[last][:].indirect(listed(groups[g])))
+        for g in range(1, count - 1):
+            nc.scalar.activation(dense[g][:], planes[last][:].indirect(listed(groups[g])), COPY)
+        nc.scalar.activation(picked[:, own, last], dense[count - 1][:], COPY)
 
         def weave(g):
-            nc.vector.tensor_copy(picked[:, groups[g], last], dense[g // 2][:, groups[g % 2]])
+            nc.vector.tensor_copy(picked[:, groups[g], last], dense[g][:])
 
         weave(0)
-        for g in range(1, 6):
+        for g in range(1, count - 1):
             weave(g)
             quantise(groups[g - 1])
-        scalar_share(last)
-        quantise(groups[5])
-        quantise(pairs[3])
+        order = list(range(count - 2)) + [count - 1, count - 2]
+        for g in order[-2:]:
+            quantise(groups[g])
 
-        chunks = spans(CHUNKS)
-        count = len(CHUNKS)
         first = keep.tile([P, S], F32, name="first")
         second = keep.tile([P, S], F32, name="second")
         third = keep.tile([P, S], F32, name="third")
-        product = {}
-        spare = count
-        for c in range(count):
-            wide = CHUNKS[c] > GROUP
-            together = 2 if wide else WEIGHTS
-            bank = psum.tile([P, together, CHUNKS[c]], F32, name="bank", tag=f"bank{c}")
-            for i in range(together):
-                product[i, c] = bank[:, i, :]
-            if wide:
-                lone = psum.tile([P, CHUNKS[c]], F32, name="lone", tag=f"bank{spare}")
-                spare = spare + 1
-                product[2, c] = lone[:]
-            for part in spans([GROUP] * (CHUNKS[c] // GROUP)):
-                cols = slice(chunks[c].start + part.start, chunks[c].start + part.stop)
-                for i in range(WEIGHTS):
-                    nc.tensor.matmul_mx(
-                        out=product[i, c][:, part],
-                        lhsT=w_codes[:, i * 2 * N : (i + 1) * 2 * N].bitcast(FP4X4),
-                        lhsT_scale=w_bytes[:, i * N : (i + 1) * N],
-                        rhs=codes[:, cols].bitcast(FP8X4),
-                        rhs_scale=scale[:, cols],
-                        start=True,
-                        stop=True,
-                    )
+        banks = {}
+        for g in order:
+            banks[g] = psum.tile([P, WEIGHTS, GROUP], F32, name="bank", tag=f"bank{g}")
+            for i in range(WEIGHTS):
+                nc.tensor.matmul_mx(
+                    out=banks[g][:, i, :],
+                    lhsT=w_codes[:, i * 2 * N : (i + 1) * 2 * N].bitcast(FP4X4),
+                    lhsT_scale=w_bytes[:, i * N : (i + 1) * N],
+                    rhs=codes[:, groups[g]].bitcast(FP8X4),
+                    rhs_scale=scale[:, groups[g]],
+                    start=True,
+                    stop=True,
+                )
 
-        def compare_first(c):
-            nc.scalar.activation(first[:, chunks[c]], product[0, c], COPY)
-            nc.vector.tensor_tensor(second[:, chunks[c]], product[1, c], first[:, chunks[c]], MAX)
-
-        def compare_last(c):
-            nc.vector.tensor_tensor(third[:, chunks[c]], product[2, c], second[:, chunks[c]], MAX)
-
-        for c in range(2):
-            compare_first(c)
-        for c in range(2):
-            compare_last(c)
-        nc.sync.dma_start(out[:, : chunks[1].stop], third[:, : chunks[1].stop])
-        for c in range(2, count + 1):
-            if c < count:
-                compare_first(c)
-            if c > 2:
-                compare_last(c - 1)
-                nc.sync.dma_start(out[:, chunks[c - 1]], third[:, chunks[c - 1]])
+        stores = {1: slice(0, 256), 3: slice(256, 512), 5: slice(512, 768), 7: groups[7], 6: groups[6]}
+        for step in range(count + 1):
+            if step < count:
+                g = order[step]
+                nc.scalar.activation(first[:, groups[g]], banks[g][:, 0, :], COPY)
+                nc.vector.tensor_tensor(second[:, groups[g]], banks[g][:, 1, :], first[:, groups[g]], MAX)
+            if step > 0:
+                g = order[step - 1]
+                nc.vector.tensor_tensor(third[:, groups[g]], banks[g][:, 2, :], second[:, groups[g]], MAX)
+                if g in stores:
+                    nc.sync.dma_start(out[:, stores[g]], third[:, stores[g]])

@@ -22,6 +22,8 @@ WEIGHTS = 3
 SCALE_ROWS = K // 32
 QUADRANTS = 4
 GROUP = 128
+LAG = 2
+WARM_UP = 256
 
 
 def spans(widths, start=0):
@@ -53,6 +55,7 @@ def tile_picked_maxout_max_e_kernel(tc, xT, w1_words, w1_scales, w2_words, w2_sc
         w_bytes = keep.tile([P, WEIGHTS * N], U8, name="w_bytes", align_bytes=64)
         staged = keep.tile([SCALE_ROWS, WEIGHTS * N], U8, name="staged", align_bytes=64)
         nc.vector.memset(w_bytes[:].bitcast(I32), 0)
+        nc.vector.memset(flat(slice(0, WARM_UP)).bitcast(I32), 0)
 
         last = PACK - 1
         nc.sync.dma_start(planes[0][:], rows[:, 0, :])
@@ -70,6 +73,17 @@ def tile_picked_maxout_max_e_kernel(tc, xT, w1_words, w1_scales, w2_words, w2_sc
         scale = keep.tile([P, S], U8, name="scale", align_bytes=64)
         groups = spans([GROUP] * (S // GROUP))
 
+        def pass_mx(target, i, rhs, rhs_scale):
+            nc.tensor.matmul_mx(
+                out=target,
+                lhsT=w_codes[:, i * 2 * N : (i + 1) * 2 * N].bitcast(FP4X4),
+                lhsT_scale=w_bytes[:, i * N : (i + 1) * N],
+                rhs=rhs.bitcast(FP8X4),
+                rhs_scale=rhs_scale,
+                start=True,
+                stop=True,
+            )
+
         def quantise(cols):
             nc.vector.quantize_mx(out=codes[:, cols].bitcast(FP8X4), scales=scale[:, cols], in_=flat(cols))
 
@@ -80,11 +94,18 @@ def tile_picked_maxout_max_e_kernel(tc, xT, w1_words, w1_scales, w2_words, w2_sc
         def dense_tile(g):
             return keep.tile([P, GROUP], BF16, name="dense", tag=f"dense{g}")
 
+        warm_codes = keep.tile([P, WARM_UP], U32, name="warm_codes", align_bytes=64)
+        warm_scale = keep.tile([P, WARM_UP], U8, name="warm_scale", align_bytes=64)
         for j in range(last):
             nc.vector.tensor_copy(picked[:, stepped, j], planes[j][:].indirect(listed(stepped)))
+            if j == 0:
+                nc.vector.quantize_mx(out=warm_codes[:].bitcast(FP8X4), scales=warm_scale[:], in_=flat(slice(0, WARM_UP)))
             early = dense_tile(count)
             nc.scalar.activation(early[:], planes[j][:].indirect(listed(own)), COPY)
             nc.scalar.activation(picked[:, own, j], early[:], COPY)
+
+        unread = psum.tile([P, WARM_UP], F32, name="unread", tag="bank0")
+        pass_mx(unread[:], WEIGHTS - 1, warm_codes[:], warm_scale[:])
 
         dense = [dense_tile(g) for g in range(count)]
         for g in (0, count - 1):
@@ -107,28 +128,33 @@ def tile_picked_maxout_max_e_kernel(tc, xT, w1_words, w1_scales, w2_words, w2_sc
         first = keep.tile([P, S], F32, name="first")
         second = keep.tile([P, S], F32, name="second")
         third = keep.tile([P, S], F32, name="third")
-        banks = {}
-        for g in order:
-            banks[g] = psum.tile([P, WEIGHTS, GROUP], F32, name="bank", tag=f"bank{g}")
-            for i in range(WEIGHTS):
-                nc.tensor.matmul_mx(
-                    out=banks[g][:, i, :],
-                    lhsT=w_codes[:, i * 2 * N : (i + 1) * 2 * N].bitcast(FP4X4),
-                    lhsT_scale=w_bytes[:, i * N : (i + 1) * N],
-                    rhs=codes[:, groups[g]].bitcast(FP8X4),
-                    rhs_scale=scale[:, groups[g]],
-                    start=True,
-                    stop=True,
-                )
+        banks = [psum.tile([P, 4, GROUP], F32, name="bank", tag=f"bank{step}") for step in range(count)]
+
+        def third_product(step):
+            later = step + LAG
+            return banks[later][:, 2, :] if later < count else banks[0][:, 2 + later - count, :]
+
+        def multiply(target, i, g):
+            pass_mx(target, i, codes[:, groups[g]], scale[:, groups[g]])
+
+        for step in range(count + LAG):
+            if step < count:
+                for i in range(2):
+                    multiply(banks[step][:, i, :], i, order[step])
+            if LAG <= step < count:
+                multiply(third_product(step - LAG), 2, order[step - LAG])
 
         stores = {1: slice(0, 256), 3: slice(256, 512), 5: slice(512, 768), 7: groups[7], 6: groups[6]}
-        for step in range(count + 1):
+        for step in range(count + LAG):
             if step < count:
                 g = order[step]
-                nc.scalar.activation(first[:, groups[g]], banks[g][:, 0, :], COPY)
-                nc.vector.tensor_tensor(second[:, groups[g]], banks[g][:, 1, :], first[:, groups[g]], MAX)
-            if step > 0:
-                g = order[step - 1]
-                nc.vector.tensor_tensor(third[:, groups[g]], banks[g][:, 2, :], second[:, groups[g]], MAX)
+                nc.scalar.activation(first[:, groups[g]], banks[step][:, 0, :], COPY)
+                nc.vector.tensor_tensor(second[:, groups[g]], banks[step][:, 1, :], first[:, groups[g]], MAX)
+            if step == 0:
+                for late in range(count - LAG, count):
+                    multiply(third_product(late), 2, order[late])
+            if step >= LAG:
+                g = order[step - LAG]
+                nc.vector.tensor_tensor(third[:, groups[g]], third_product(step - LAG), second[:, groups[g]], MAX)
                 if g in stores:
                     nc.sync.dma_start(out[:, stores[g]], third[:, stores[g]])

@@ -23,7 +23,6 @@ SCALE_ROWS = K // 32
 QUADRANTS = 4
 GROUP = 128
 LAG = 2
-WARM_UP = 256
 
 
 def spans(widths, start=0):
@@ -55,7 +54,6 @@ def tile_picked_maxout_max_e_kernel(tc, xT, w1_words, w1_scales, w2_words, w2_sc
         w_bytes = keep.tile([P, WEIGHTS * N], U8, name="w_bytes", align_bytes=64)
         staged = keep.tile([SCALE_ROWS, WEIGHTS * N], U8, name="staged", align_bytes=64)
         nc.vector.memset(w_bytes[:].bitcast(I32), 0)
-        nc.vector.memset(flat(slice(0, WARM_UP)).bitcast(I32), 0)
 
         last = PACK - 1
         nc.sync.dma_start(planes[0][:], rows[:, 0, :])
@@ -94,18 +92,11 @@ def tile_picked_maxout_max_e_kernel(tc, xT, w1_words, w1_scales, w2_words, w2_sc
         def dense_tile(g):
             return keep.tile([P, GROUP], BF16, name="dense", tag=f"dense{g}")
 
-        warm_codes = keep.tile([P, WARM_UP], U32, name="warm_codes", align_bytes=64)
-        warm_scale = keep.tile([P, WARM_UP], U8, name="warm_scale", align_bytes=64)
         for j in range(last):
             nc.vector.tensor_copy(picked[:, stepped, j], planes[j][:].indirect(listed(stepped)))
-            if j == 0:
-                nc.vector.quantize_mx(out=warm_codes[:].bitcast(FP8X4), scales=warm_scale[:], in_=flat(slice(0, WARM_UP)))
             early = dense_tile(count)
             nc.scalar.activation(early[:], planes[j][:].indirect(listed(own)), COPY)
             nc.scalar.activation(picked[:, own, j], early[:], COPY)
-
-        unread = psum.tile([P, WARM_UP], F32, name="unread", tag="bank0")
-        pass_mx(unread[:], WEIGHTS - 1, warm_codes[:], warm_scale[:])
 
         dense = [dense_tile(g) for g in range(count)]
         for g in (0, count - 1):

@@ -62,10 +62,20 @@ def tile_picked_maxout_max_e_kernel(tc, xT, w1_words, w1_scales, w2_words, w2_sc
             nc.sync.dma_start(staged[:, i * N : (i + 1) * N].bitcast(I32), scale_rows[0].bitcast(I32))
         for j in range(1, PACK):
             nc.sync.dma_start(planes[j][:], rows[:, j, :])
-        for i, words in enumerate((w1_words, w2_words, w3_words)):
+
+        def load_codes(i):
+            words = (w1_words, w2_words, w3_words)[i]
             nc.sync.dma_start(w_codes[:, i * 2 * N : (i + 1) * 2 * N].bitcast(I32), words[0].bitcast(I32))
-        for q in range(QUADRANTS):
+
+        def move_scales(q):
             nc.sync.dma_start(w_bytes[32 * q : 32 * q + 4, :].bitcast(I32), staged[4 * q : 4 * q + 4, :].bitcast(I32))
+
+        for q in range(QUADRANTS):
+            if q == QUADRANTS // 2:
+                load_codes(0)
+            move_scales(q)
+        for i in range(1, WEIGHTS):
+            load_codes(i)
 
         codes = keep.tile([P, S], U32, name="codes", align_bytes=64)
         scale = keep.tile([P, S], U8, name="scale", align_bytes=64)
@@ -128,12 +138,11 @@ def tile_picked_maxout_max_e_kernel(tc, xT, w1_words, w1_scales, w2_words, w2_sc
         def multiply(target, i, g):
             pass_mx(target, i, codes[:, groups[g]], scale[:, groups[g]])
 
-        for step in range(count + LAG):
-            if step < count:
-                for i in range(2):
-                    multiply(banks[step][:, i, :], i, order[step])
-            if LAG <= step < count:
+        for step in range(count):
+            if step >= LAG:
                 multiply(third_product(step - LAG), 2, order[step - LAG])
+            for i in (0, 1) if step == 0 else (1, 0):
+                multiply(banks[step][:, i, :], i, order[step])
 
         stores = {1: slice(0, 256), 3: slice(256, 512), 5: slice(512, 768), 7: groups[7], 6: groups[6]}
         for step in range(count + LAG):

@@ -22,7 +22,7 @@ WEIGHTS = 3
 SCALE_ROWS = K // 32
 QUADRANTS = 4
 GROUP = 128
-LAG = 2
+AHEAD = 3
 
 
 def spans(widths, start=0):
@@ -132,29 +132,41 @@ def tile_picked_maxout_max_e_kernel(tc, xT, w1_words, w1_scales, w2_words, w2_sc
         banks = [psum.tile([P, 4, GROUP], F32, name="bank", tag=f"bank{step}") for step in range(count)]
 
         def third_product(step):
-            later = step + LAG
-            return banks[later][:, 2, :] if later < count else banks[0][:, 2 + later - count, :]
+            if step < 2:
+                return banks[2][:, 2 + step, :]
+            return banks[(step + 1) % count][:, 2, :]
 
         def multiply(target, i, g):
             pass_mx(target, i, codes[:, groups[g]], scale[:, groups[g]])
 
         for step in range(count):
-            if step >= LAG:
-                multiply(third_product(step - LAG), 2, order[step - LAG])
+            if step == 2:
+                both = slice(0, 2 * GROUP)
+                pass_mx(banks[2][:, 2:4, :].rearrange("p a n -> p (a n)"), 2, codes[:, both], scale[:, both])
+            if step > 2:
+                multiply(third_product(step - 1), 2, order[step - 1])
             for i in (0, 1) if step == 0 else (1, 0):
                 multiply(banks[step][:, i, :], i, order[step])
 
-        stores = {1: slice(0, 256), 3: slice(256, 512), 5: slice(512, 768), 7: groups[7], 6: groups[6]}
-        for step in range(count + LAG):
-            if step < count:
-                g = order[step]
-                nc.scalar.activation(first[:, groups[g]], banks[step][:, 0, :], COPY)
-                nc.vector.tensor_tensor(second[:, groups[g]], banks[step][:, 1, :], first[:, groups[g]], MAX)
-            if step == 0:
-                for late in range(count - LAG, count):
-                    multiply(third_product(late), 2, order[late])
-            if step >= LAG:
-                g = order[step - LAG]
-                nc.vector.tensor_tensor(third[:, groups[g]], third_product(step - LAG), second[:, groups[g]], MAX)
-                if g in stores:
-                    nc.sync.dma_start(out[:, stores[g]], third[:, stores[g]])
+        def compare_first(step):
+            g = order[step]
+            nc.scalar.activation(first[:, groups[g]], banks[step][:, 0, :], COPY)
+            nc.vector.tensor_tensor(second[:, groups[g]], banks[step][:, 1, :], first[:, groups[g]], MAX)
+
+        stores = {1: slice(0, 256), 3: slice(256, 512), 4: groups[4], 5: groups[5], 7: groups[7], 6: groups[6]}
+
+        def compare_last(step):
+            g = order[step]
+            nc.vector.tensor_tensor(third[:, groups[g]], third_product(step), second[:, groups[g]], MAX)
+            if g in stores:
+                nc.sync.dma_start(out[:, stores[g]], third[:, stores[g]])
+
+        for step in range(AHEAD):
+            compare_first(step)
+        multiply(third_product(count - 1), 2, order[count - 1])
+        for step in range(AHEAD - 1):
+            compare_last(step)
+        for step in range(AHEAD, count):
+            compare_first(step)
+            compare_last(step - 1)
+        compare_last(count - 1)

@@ -23,6 +23,7 @@ SCALE_ROWS = K // 32
 QUADRANTS = 4
 GROUP = 128
 AHEAD = 3
+OWN = 192
 
 
 def spans(widths, start=0):
@@ -96,7 +97,8 @@ def tile_picked_maxout_max_e_kernel(tc, xT, w1_words, w1_scales, w2_words, w2_sc
             nc.vector.quantize_mx(out=codes[:, cols].bitcast(FP8X4), scales=scale[:, cols], in_=flat(cols))
 
         count = len(groups)
-        own = groups[count - 1]
+        own = slice(S - OWN, S)
+        shared = own.start - groups[count - 2].start
         stepped = slice(0, own.start)
 
         def dense_tile(g):
@@ -104,7 +106,7 @@ def tile_picked_maxout_max_e_kernel(tc, xT, w1_words, w1_scales, w2_words, w2_sc
 
         for j in range(last):
             nc.vector.tensor_copy(picked[:, stepped, j], planes[j][:].indirect(listed(stepped)))
-            early = dense_tile(count)
+            early = keep.tile([P, OWN], BF16, name="early", tag="early")
             nc.scalar.activation(early[:], planes[j][:].indirect(listed(own)), COPY)
             nc.scalar.activation(picked[:, own, j], early[:], COPY)
 
@@ -113,10 +115,12 @@ def tile_picked_maxout_max_e_kernel(tc, xT, w1_words, w1_scales, w2_words, w2_sc
             nc.vector.tensor_copy(dense[g][:], planes[last][:].indirect(listed(groups[g])))
         for g in range(1, count - 1):
             nc.scalar.activation(dense[g][:], planes[last][:].indirect(listed(groups[g])), COPY)
-        nc.scalar.activation(picked[:, own, last], dense[count - 1][:], COPY)
+        nc.scalar.activation(picked[:, groups[count - 1], last], dense[count - 1][:], COPY)
+        nc.scalar.activation(picked[:, own.start : groups[count - 1].start, last], dense[count - 2][:, shared:], COPY)
 
         def weave(g):
-            nc.vector.tensor_copy(picked[:, groups[g], last], dense[g][:])
+            width = shared if g == count - 2 else GROUP
+            nc.vector.tensor_copy(picked[:, groups[g].start : groups[g].start + width, last], dense[g][:, :width])
 
         weave(0)
         for g in range(1, count - 1):
@@ -148,16 +152,23 @@ def tile_picked_maxout_max_e_kernel(tc, xT, w1_words, w1_scales, w2_words, w2_sc
             for i in (0, 1) if step == 0 else (1, 0):
                 multiply(banks[step][:, i, :], i, order[step])
 
+        def parts(step):
+            return spans([GROUP // 2] * 2) if step == count - 1 else spans([GROUP])
+
         def compare_first(step):
             g = order[step]
             nc.scalar.activation(first[:, groups[g]], banks[step][:, 0, :], COPY)
-            nc.vector.tensor_tensor(second[:, groups[g]], banks[step][:, 1, :], first[:, groups[g]], MAX)
+            for part in parts(step):
+                cols = slice(groups[g].start + part.start, groups[g].start + part.stop)
+                nc.vector.tensor_tensor(second[:, cols], banks[step][:, 1, part], first[:, cols], MAX)
 
         stores = {1: slice(0, 256), 3: slice(256, 512), 4: groups[4], 5: groups[5], 7: groups[7], 6: groups[6]}
 
         def compare_last(step):
             g = order[step]
-            nc.vector.tensor_tensor(third[:, groups[g]], third_product(step), second[:, groups[g]], MAX)
+            for part in parts(step):
+                cols = slice(groups[g].start + part.start, groups[g].start + part.stop)
+                nc.vector.tensor_tensor(third[:, cols], third_product(step)[:, part], second[:, cols], MAX)
             if g in stores:
                 nc.sync.dma_start(out[:, stores[g]], third[:, stores[g]])
 

@@ -23,7 +23,7 @@ SCALE_ROWS = K // 32
 QUADRANTS = 4
 GROUP = 128
 AHEAD = 3
-OWN = 192
+OWN = 128
 
 
 def spans(widths, start=0):
@@ -71,12 +71,10 @@ def tile_picked_maxout_max_e_kernel(tc, xT, w1_words, w1_scales, w2_words, w2_sc
         def move_scales(q):
             nc.sync.dma_start(w_bytes[32 * q : 32 * q + 4, :].bitcast(I32), staged[4 * q : 4 * q + 4, :].bitcast(I32))
 
-        for q in range(QUADRANTS):
-            if q == QUADRANTS // 2:
-                load_codes(0)
-            move_scales(q)
-        for i in range(1, WEIGHTS):
+        for i in range(WEIGHTS):
             load_codes(i)
+        for q in range(QUADRANTS):
+            move_scales(q)
 
         codes = keep.tile([P, S], U32, name="codes", align_bytes=64)
         scale = keep.tile([P, S], U8, name="scale", align_bytes=64)
@@ -98,7 +96,6 @@ def tile_picked_maxout_max_e_kernel(tc, xT, w1_words, w1_scales, w2_words, w2_sc
 
         count = len(groups)
         own = slice(S - OWN, S)
-        shared = own.start - groups[count - 2].start
         stepped = slice(0, own.start)
 
         def dense_tile(g):
@@ -116,11 +113,9 @@ def tile_picked_maxout_max_e_kernel(tc, xT, w1_words, w1_scales, w2_words, w2_sc
         for g in range(1, count - 1):
             nc.scalar.activation(dense[g][:], planes[last][:].indirect(listed(groups[g])), COPY)
         nc.scalar.activation(picked[:, groups[count - 1], last], dense[count - 1][:], COPY)
-        nc.scalar.activation(picked[:, own.start : groups[count - 1].start, last], dense[count - 2][:, shared:], COPY)
 
         def weave(g):
-            width = shared if g == count - 2 else GROUP
-            nc.vector.tensor_copy(picked[:, groups[g].start : groups[g].start + width, last], dense[g][:, :width])
+            nc.vector.tensor_copy(picked[:, groups[g], last], dense[g][:])
 
         weave(0)
         for g in range(1, count - 1):
@@ -133,48 +128,60 @@ def tile_picked_maxout_max_e_kernel(tc, xT, w1_words, w1_scales, w2_words, w2_sc
         first = keep.tile([P, S], F32, name="first")
         second = keep.tile([P, S], F32, name="second")
         third = keep.tile([P, S], F32, name="third")
-        banks = [psum.tile([P, 4, GROUP], F32, name="bank", tag=f"bank{step}") for step in range(count)]
+        APART = 4
+        where = {}
 
-        def third_product(step):
-            if step < 2:
-                return banks[2][:, 2 + step, :]
-            return banks[(step + 1) % count][:, 2, :]
+        def bank(tag, *products):
+            tile = psum.tile([P, len(products), GROUP], F32, name="bank", tag=f"bank{tag}")
+            for slot, product in enumerate(products):
+                where[product] = tile[:, slot, :]
+            return tile
 
-        def multiply(target, i, g):
-            pass_mx(target, i, codes[:, groups[g]], scale[:, groups[g]])
+        def multiply(*products):
+            for i, step in products:
+                pass_mx(where[i, step], i, codes[:, groups[order[step]]], scale[:, groups[order[step]]])
 
-        for step in range(count):
-            if step == 2:
-                both = slice(0, 2 * GROUP)
-                pass_mx(banks[2][:, 2:4, :].rearrange("p a n -> p (a n)"), 2, codes[:, both], scale[:, both])
-            if step > 2:
-                multiply(third_product(step - 1), 2, order[step - 1])
-            for i in (0, 1) if step == 0 else (1, 0):
-                multiply(banks[step][:, i, :], i, order[step])
-
-        def parts(step):
-            return spans([GROUP // 2] * 2) if step == count - 1 else spans([GROUP])
+        def copy_out(step):
+            nc.scalar.activation(first[:, groups[order[step]]], where[0, step], COPY)
 
         def compare_first(step):
             g = order[step]
-            nc.scalar.activation(first[:, groups[g]], banks[step][:, 0, :], COPY)
-            for part in parts(step):
-                cols = slice(groups[g].start + part.start, groups[g].start + part.stop)
-                nc.vector.tensor_tensor(second[:, cols], banks[step][:, 1, part], first[:, cols], MAX)
+            nc.vector.tensor_tensor(second[:, groups[g]], where[1, step], first[:, groups[g]], MAX)
+
+        for step in range(2):
+            bank(step, (0, step), (1, step))
+            multiply((0, step), (1, step))
+            copy_out(step)
+            compare_first(step)
+        both = slice(0, 2 * GROUP)
+        shared = bank(2, (2, 0), (2, 1), (1, 2), (0, 2))
+        pass_mx(shared[:, 0:2, :].rearrange("p a n -> p (a n)"), 2, codes[:, both], scale[:, both])
+        multiply((0, 2), (1, 2))
+        copy_out(2)
+        bank(3, (2, 2), (1, 3), (0, 3))
+        multiply((2, 2), (0, 3), (1, 3))
+        copy_out(3)
+        bank(6, (0, APART))
+        multiply((0, APART))
+        copy_out(APART)
+        for step in range(APART, count - 1):
+            bank(6 + (step + 1) % 2, (0, step + 1))
+            multiply((0, step + 1))
+            copy_out(step + 1)
+            bank(step % 6, (2, step - 1), (1, step))
+            multiply((2, step - 1), (1, step))
+        bank(1, (2, count - 2), (1, count - 1), (2, count - 1))
+        multiply((2, count - 2), (1, count - 1), (2, count - 1))
 
         stores = {1: slice(0, 256), 3: slice(256, 512), 4: groups[4], 5: groups[5], 7: groups[7], 6: groups[6]}
 
         def compare_last(step):
             g = order[step]
-            for part in parts(step):
-                cols = slice(groups[g].start + part.start, groups[g].start + part.stop)
-                nc.vector.tensor_tensor(third[:, cols], third_product(step)[:, part], second[:, cols], MAX)
+            nc.vector.tensor_tensor(third[:, groups[g]], where[2, step], second[:, groups[g]], MAX)
             if g in stores:
                 nc.sync.dma_start(out[:, stores[g]], third[:, stores[g]])
 
-        for step in range(AHEAD):
-            compare_first(step)
-        multiply(third_product(count - 1), 2, order[count - 1])
+        compare_first(2)
         for step in range(AHEAD - 1):
             compare_last(step)
         for step in range(AHEAD, count):

@@ -42,7 +42,7 @@ def tile_picked_maxout_max_e_kernel(tc, xT, w1_words, w1_scales, w2_words, w2_sc
         psum = ctx.enter_context(tc.psum_pool(name="psum", bufs=1))
 
         offsets = keep.tile([P, S // 16], U16, name="offsets")
-        planes = [keep.tile([P, T], F32, name=f"plane{j}", tag=f"plane{j}") for j in range(PACK)]
+        planes = [keep.tile([P, T], F32, name=f"plane{j}", tag=f"plane{j}", align_bytes=256) for j in range(PACK)]
         picked = keep.tile([P, S, PACK], BF16, name="picked", align_bytes=64)
 
         def listed(entries):

@@ -173,7 +173,7 @@ def tile_picked_maxout_max_e_kernel(tc, xT, w1_words, w1_scales, w2_words, w2_sc
         bank(1, (2, count - 2), (1, count - 1), (2, count - 1))
         multiply((2, count - 2), (1, count - 1), (2, count - 1))
 
-        stores = {1: slice(0, 256), 3: slice(256, 512), 4: groups[4], 5: groups[5], 7: groups[7], 6: groups[6]}
+        stores = dict(enumerate(groups))
 
         def compare_last(step):
             g = order[step]

@@ -179,7 +179,7 @@ def tile_picked_maxout_max_e_kernel(tc, xT, w1_words, w1_scales, w2_words, w2_sc
             g = order[step]
             nc.vector.tensor_tensor(third[:, groups[g]], where[2, step], second[:, groups[g]], MAX)
             if g in stores:
-                nc.sync.dma_start(out[:, stores[g]], third[:, stores[g]])
+                (nc.scalar if step in (count - 4, count - 2) else nc.sync).dma_start(out[:, stores[g]], third[:, stores[g]])
 
         compare_first(2)
         for step in range(AHEAD - 1):

from contextlib import ExitStack

import concourse.mybir as mybir

K, T, S, N = 512, 4096, 1024, 128
FLOPS = 2 * 3 * K * N * S

F32 = mybir.dt.float32
BF16 = mybir.dt.bfloat16
I32 = mybir.dt.int32
U32 = mybir.dt.uint32
U16 = mybir.dt.uint16
U8 = mybir.dt.uint8
FP8X4 = mybir.dt.float8_e4m3fn_x4
FP4X4 = mybir.dt.float4_e2m1fn_x4
COPY = mybir.ActivationFunctionType.Copy
MAX = mybir.AluOpType.max

P = 128
PACK = 4
WEIGHTS = 3
SCALE_ROWS = K // 32
QUADRANTS = 4
GROUP = 128
AHEAD = 3
OWN = 128


def spans(widths, start=0):
    result = []
    for width in widths:
        result.append(slice(start, start + width))
        start = start + width
    return result


def tile_picked_maxout_max_e_kernel(tc, xT, w1_words, w1_scales, w2_words, w2_scales, w3_words, w3_scales, offs, out):
    nc = tc.nc
    rows = xT.rearrange("(p j) t -> p j t", j=PACK)
    with ExitStack() as ctx:
        keep = ctx.enter_context(tc.tile_pool(name="keep", bufs=1))
        psum = ctx.enter_context(tc.psum_pool(name="psum", bufs=1))

        offsets = keep.tile([P, S // 16], U16, name="offsets")
        planes = [keep.tile([P, T], F32, name=f"plane{j}", tag=f"plane{j}", align_bytes=256) for j in range(PACK)]
        picked = keep.tile([P, S, PACK], BF16, name="picked", align_bytes=64)

        def listed(entries):
            return offsets[:, entries.start // 16 : entries.stop // 16]

        def flat(entries):
            return picked[:, entries, :].rearrange("p n j -> p (n j)")

        w_codes = keep.tile([P, WEIGHTS * 2 * N], U8, name="w_codes", align_bytes=64)
        w_bytes = keep.tile([P, WEIGHTS * N], U8, name="w_bytes", align_bytes=64)
        staged = keep.tile([SCALE_ROWS, WEIGHTS * N], U8, name="staged", align_bytes=64)
        nc.vector.memset(w_bytes[:].bitcast(I32), 0)

        last = PACK - 1
        nc.sync.dma_start(planes[0][:], rows[:, 0, :])
        nc.sync.dma_start(offsets[:], offs)
        for i, scale_rows in enumerate((w1_scales, w2_scales, w3_scales)):
            nc.sync.dma_start(staged[:, i * N : (i + 1) * N].bitcast(I32), scale_rows[0].bitcast(I32))
        for j in range(1, PACK):
            nc.sync.dma_start(planes[j][:], rows[:, j, :])

        def load_codes(i):
            words = (w1_words, w2_words, w3_words)[i]
            nc.sync.dma_start(w_codes[:, i * 2 * N : (i + 1) * 2 * N].bitcast(I32), words[0].bitcast(I32))

        def move_scales(q):
            nc.sync.dma_start(w_bytes[32 * q : 32 * q + 4, :].bitcast(I32), staged[4 * q : 4 * q + 4, :].bitcast(I32))

        for i in range(WEIGHTS):
            load_codes(i)
        for q in range(QUADRANTS):
            move_scales(q)

        codes = keep.tile([P, S], U32, name="codes", align_bytes=64)
        scale = keep.tile([P, S], U8, name="scale", align_bytes=64)
        groups = spans([GROUP] * (S // GROUP))

        def pass_mx(target, i, rhs, rhs_scale):
            nc.tensor.matmul_mx(
                out=target,
                lhsT=w_codes[:, i * 2 * N : (i + 1) * 2 * N].bitcast(FP4X4),
                lhsT_scale=w_bytes[:, i * N : (i + 1) * N],
                rhs=rhs.bitcast(FP8X4),
                rhs_scale=rhs_scale,
                start=True,
                stop=True,
            )

        def quantise(cols):
            nc.vector.quantize_mx(out=codes[:, cols].bitcast(FP8X4), scales=scale[:, cols], in_=flat(cols))

        count = len(groups)
        own = slice(S - OWN, S)
        stepped = slice(0, own.start)

        def dense_tile(g):
            return keep.tile([P, GROUP], BF16, name="dense", tag=f"dense{g}")

        for j in range(last):
            nc.vector.tensor_copy(picked[:, stepped, j], planes[j][:].indirect(listed(stepped)))
            early = keep.tile([P, OWN], BF16, name="early", tag="early")
            nc.scalar.activation(early[:], planes[j][:].indirect(listed(own)), COPY)
            nc.scalar.activation(picked[:, own, j], early[:], COPY)

        dense = [dense_tile(g) for g in range(count)]
        for g in (0, count - 1):
            nc.vector.tensor_copy(dense[g][:], planes[last][:].indirect(listed(groups[g])))
        for g in range(1, count - 1):
            nc.scalar.activation(dense[g][:], planes[last][:].indirect(listed(groups[g])), COPY)
        nc.scalar.activation(picked[:, groups[count - 1], last], dense[count - 1][:], COPY)

        def weave(g):
            nc.vector.tensor_copy(picked[:, groups[g], last], dense[g][:])

        weave(0)
        for g in range(1, count - 1):
            weave(g)
            quantise(groups[g - 1])
        order = list(range(count - 2)) + [count - 1, count - 2]
        for g in order[-2:]:
            quantise(groups[g])

        first = keep.tile([P, S], F32, name="first")
        second = keep.tile([P, S], F32, name="second")
        third = keep.tile([P, S], F32, name="third")
        APART = 4
        where = {}

        def bank(tag, *products):
            tile = psum.tile([P, len(products), GROUP], F32, name="bank", tag=f"bank{tag}")
            for slot, product in enumerate(products):
                where[product] = tile[:, slot, :]
            return tile

        def multiply(*products):
            for i, step in products:
                pass_mx(where[i, step], i, codes[:, groups[order[step]]], scale[:, groups[order[step]]])

        def copy_out(step):
            nc.scalar.activation(first[:, groups[order[step]]], where[0, step], COPY)

        def compare_first(step):
            g = order[step]
            nc.vector.tensor_tensor(second[:, groups[g]], where[1, step], first[:, groups[g]], MAX)

        for step in range(2):
            bank(step, (0, step), (1, step))
            multiply((0, step), (1, step))
            copy_out(step)
            compare_first(step)
        both = slice(0, 2 * GROUP)
        shared = bank(2, (2, 0), (2, 1), (1, 2), (0, 2))
        pass_mx(shared[:, 0:2, :].rearrange("p a n -> p (a n)"), 2, codes[:, both], scale[:, both])
        multiply((0, 2), (1, 2))
        copy_out(2)
        bank(3, (2, 2), (1, 3), (0, 3))
        multiply((2, 2), (0, 3), (1, 3))
        copy_out(3)
        bank(6, (0, APART))
        multiply((0, APART))
        copy_out(APART)
        for step in range(APART, count - 1):
            bank(6 + (step + 1) % 2, (0, step + 1))
            multiply((0, step + 1))
            copy_out(step + 1)
            bank(step % 6, (2, step - 1), (1, step))
            multiply((2, step - 1), (1, step))
        bank(1, (2, count - 2), (1, count - 1), (2, count - 1))
        multiply((2, count - 2), (1, count - 1), (2, count - 1))

        stores = dict(enumerate(groups))

        def compare_last(step):
            g = order[step]
            nc.vector.tensor_tensor(third[:, groups[g]], where[2, step], second[:, groups[g]], MAX)
            if g in stores:
                (nc.scalar if step in (count - 4, count - 2) else nc.sync).dma_start(out[:, stores[g]], third[:, stores[g]])

        compare_first(2)
        for step in range(AHEAD - 1):
            compare_last(step)
        for step in range(AHEAD, count):
            compare_first(step)
            compare_last(step - 1)
        compare_last(count - 1)
